import numpy as np
import ml_dtypes


def mxq(x, axis, fmt="e4m3"):
    dtype, down = {"e4m3": (ml_dtypes.float8_e4m3fn, 7), "e5m2": (ml_dtypes.float8_e5m2, 14)}[fmt]
    v = np.moveaxis(np.asarray(x, np.float32).astype(ml_dtypes.bfloat16).astype(np.float64), axis, -1)
    blocks = v.reshape(v.shape[:-1] + (-1, 32))
    amax = np.abs(blocks).max(-1, keepdims=True)
    byte = np.maximum(np.where(amax > 0, np.frexp(amax)[1] - 1 + 127, 0) - down, 1)
    scale = np.exp2(byte - 127.0)
    codes = (blocks / scale).astype(np.float32).astype(dtype).astype(np.float64)
    return np.moveaxis((codes * scale).reshape(v.shape), -1, axis)


WIDE = False


def mx_kscale(k):
    if not WIDE:
        return np.ones(k)
    levels = np.array([10, -10, 5, -5, 0])
    if k % 512:
        return np.exp2(np.random.permutation(np.resize(levels, k // 32))).repeat(32)
    a = np.empty((k // 512, 16))
    for p in range(k // 512):
        a[p, :8] = np.random.permutation(np.resize(levels, 8))
        for g in range(8):
            far = levels[np.abs(levels - a[p, g]) >= 10]
            a[p, g + 8] = far[np.random.randint(len(far))]
    return np.exp2(a.ravel()).repeat(32)


def f64(x):
    return np.asarray(x).astype(np.float64)


def striped(idx):
    return np.tile(np.asarray(idx).reshape(-1, 16).T, (8, 1)).astype(np.uint16)


def unstriped(offs):
    return offs[:16].T.reshape(-1).astype(np.int64)


E2M1 = np.array([0.0, 0.5, 1.0, 1.5, 2.0, 3.0, 4.0, 6.0, -0.0, -0.5, -1.0, -1.5, -2.0, -3.0, -4.0, -6.0])


def pack_weight(w, fmt):
    k, n = w.shape
    w = f64(np.asarray(w, np.float32).astype(ml_dtypes.bfloat16)).reshape(k // 32, 32, n)
    amax = np.abs(w).max(1)
    if fmt == "e4m3":
        byte = np.frexp(amax)[1] - 1 + 127 - 7
    else:
        mant, ex = np.frexp(amax / 6.0)
        byte = np.where(mant > 0.5, ex, ex - 1) + 127
    byte = np.clip(np.where(amax > 0, byte, 1), 1, 254)
    scaled = (w * np.exp2(127.0 - byte)[:, None, :]).reshape(k, n).astype(np.float32)
    by_word = np.ascontiguousarray(scaled.reshape(k // 512, 128, 4, n).transpose(0, 1, 3, 2))
    if fmt == "e4m3":
        words = by_word.astype(ml_dtypes.float8_e4m3fn).view(np.uint8)
    else:
        c = by_word.astype(ml_dtypes.float4_e2m1fn).view(np.uint8) & 0xF
        words = (c[..., 0::2] | (c[..., 1::2] << 4)).reshape(k // 512, 128, 2 * n)
    return np.ascontiguousarray(words), np.ascontiguousarray(byte.astype(np.uint8).reshape(k // 512, 16, n))


def unpack_weight(words, scales, fmt):
    g, _, n = scales.shape
    words = np.ascontiguousarray(words).reshape(g, 128, n, -1)
    if fmt == "e4m3":
        vals = words.view(ml_dtypes.float8_e4m3fn).astype(np.float64)
    else:
        nib = np.empty((g, 128, n, 4), np.uint8)
        nib[..., 0::2] = words & 0xF
        nib[..., 1::2] = words >> 4
        vals = E2M1[nib]
    vals = vals * np.repeat(np.exp2(scales.astype(np.float64) - 127.0), 8, axis=1)[..., None]
    return vals.transpose(0, 1, 3, 2).reshape(g * 512, n)


B, N, T, D, NQ = 2, 512, 2048, 512, 128


def setup_inputs():
    n = np.random.standard_normal
    jdx = np.random.permutation(1024)[:B * NQ]
    pages = np.random.permutation(T // 64)[:B * N // 64]
    idx = (pages[:, None] * 64 + np.arange(64)[None, :]).reshape(-1)
    s = mx_kscale(D)[:, None]
    kp = pack_weight(n((D, T)) / s, "e4m3")
    return {
        "qT": (n((D, 1024)) * s * (1.00 / np.sqrt(D))).astype(np.float32),
        "k_words": kp[0],
        "k_scales": kp[1],
        "kb": np.tile(n(2048), (128, 1)).astype(np.float32),
        "offq": striped(jdx),
        "offs": striped(idx),
    }


def reference(qT, k_words, k_scales, kb, offq, offs):
    jdx = unstriped(offq)
    idx = unstriped(offs)
    pick = lambda x, which: x[:, which].reshape(x.shape[0], B, -1).transpose(1, 0, 2)
    qg = mxq(pick(f64(qT), jdx), 1, "e4m3")
    k = unpack_weight(k_words, k_scales, "e4m3")
    kg = pick(k, idx)
    qq = qg
    a = qq.transpose(0, 2, 1) @ kg
    y = a + pick(f64(kb), idx)[:, :1, :]
    return y

@@ -1,0 +1,98 @@
+from contextlib import ExitStack
+
+import concourse.mybir as mybir
+from concourse.masks import make_identity
+
+B, N, T, D, NQ, TQ = 2, 512, 2048, 512, 128, 1024
+P = 128
+PACK = 4
+FLOPS = 2 * B * NQ * N * D
+BYTES = 4 * D * TQ + D * T + 16 * T + 4 * T + 2 * P * (B * NQ + B * N) // 16 + 4 * B * NQ * N
+
+F32 = mybir.dt.float32
+BF16 = mybir.dt.bfloat16
+I32 = mybir.dt.int32
+U32 = mybir.dt.uint32
+U16 = mybir.dt.uint16
+U8 = mybir.dt.uint8
+FP8X4 = mybir.dt.float8_e4m3fn_x4
+ADD = mybir.AluOpType.add
+
+
+def tile_attend_lq_score_kernel(tc, qT, k_words, k_scales, kb, offq, offs, out):
+    nc = tc.nc
+    with ExitStack() as ctx:
+        sb = ctx.enter_context(tc.tile_pool(name="sb", bufs=1))
+        ps = ctx.enter_context(tc.psum_pool(name="ps", bufs=1))
+
+        key_list = sb.tile([P, B * N // 16], U16, name="key_list")
+        query_list = sb.tile([P, B * NQ // 16], U16, name="query_list")
+        q_planes = [sb.tile([P, TQ], F32, name="q_plane%d" % t) for t in range(PACK)]
+        word_pool = sb.tile([P, T], I32, name="word_pool")
+        scale_pool = sb.tile([P, T // 4], I32, name="scale_pool")
+        bias_pool = sb.tile([P, T], F32, name="bias_pool")
+        ident = sb.tile([P, P], F32, name="ident")
+
+        nc.vector.memset(scale_pool[:], 0)
+        nc.vector.memset(bias_pool[0 : P - 1, :], 0.0)
+        make_identity(nc, ident[:])
+
+        q_rows = qT.rearrange("(p t) n -> p t n", t=PACK)
+        nc.sync.dma_start(key_list[:], offs)
+        nc.scalar.dma_start(bias_pool[P - 1 : P, :], kb[0:1, :])
+        nc.sync.dma_start(q_planes[0][:], q_rows[:, 0, :])
+        nc.sync.dma_start(query_list[:], offq)
+        for t in range(1, PACK):
+            nc.sync.dma_start(q_planes[t][:], q_rows[:, t, :])
+        nc.sync.dma_start(word_pool[:], k_words[0].rearrange("p t r -> p (t r)").bitcast(I32))
+        for quad in range(4):
+            nc.scalar.dma_start(
+                scale_pool[32 * quad : 32 * quad + 4, :], k_scales[0, 4 * quad : 4 * quad + 4, :].bitcast(I32)
+            )
+
+        bias_row = sb.tile([P, B * N], F32, name="bias_row")
+        nc.vector.tensor_copy(bias_row[:], bias_pool[:].indirect(key_list[:]))
+        bias_col = sb.tile([P, B * N // P], F32, name="bias_col")
+        for b in range(B):
+            turned = ps.tile([P, 4, P], F32, name="turned%d" % b)
+            for c in range(4):
+                nc.tensor.transpose(turned[:, c, :], bias_row[:, b * N + c * P : b * N + (c + 1) * P], ident[:])
+            nc.scalar.copy(bias_col[:, 4 * b : 4 * b + 4], turned[:, :, P - 1])
+        bias = []
+        for b in range(B):
+            spread = ps.tile([P, 4, P], F32, name="spread%d" % b)
+            for c in range(4):
+                nc.tensor.transpose(spread[:, c, :], bias_col[:, 4 * b + c : 4 * b + c + 1].to_broadcast([P, P]), ident[:])
+            bias_b = sb.tile([P, N], F32, name="bias%d" % b)
+            nc.scalar.copy(bias_b[:], spread[:].rearrange("p c n -> p (c n)"))
+            bias.append(bias_b)
+
+        q_grouped = sb.tile([P, B * NQ, PACK], BF16, name="q_grouped", align_bytes=64)
+        key_scales = sb.tile([P, B * N], U8, name="key_scales", align_bytes=64)
+        nc.vector.tensor_copy(q_grouped[:, :, 0], q_planes[0][:].indirect(query_list[:]))
+        nc.vector.tensor_copy(key_scales[:], scale_pool[:].bitcast(U8).indirect(key_list[:]))
+        for t in range(1, PACK):
+            nc.vector.tensor_copy(q_grouped[:, :, t], q_planes[t][:].indirect(query_list[:]))
+        q_codes = sb.tile([P, B * NQ], U32, name="q_codes", align_bytes=64)
+        q_scales = sb.tile([P, B * NQ], U8, name="q_scales", align_bytes=64)
+        nc.vector.quantize_mx(out=q_codes[:].bitcast(FP8X4), scales=q_scales[:], in_=q_grouped[:].rearrange("p n t -> p (n t)"))
+
+        scores = []
+        for b in range(B):
+            key_words = sb.tile([P, N], U32, name="key_words%d" % b, align_bytes=64)
+            nc.vector.tensor_copy(key_words[:], word_pool[:].bitcast(U32).indirect(key_list[:, b * N // 16 : (b + 1) * N // 16]))
+            acc = ps.tile([P, N], F32, name="scores%d" % b)
+            nc.tensor.matmul_mx(
+                out=acc[:],
+                lhsT=q_codes[:, b * NQ : (b + 1) * NQ].bitcast(FP8X4),
+                lhsT_scale=q_scales[:, b * NQ : (b + 1) * NQ],
+                rhs=key_words[:].bitcast(FP8X4),
+                rhs_scale=key_scales[:, b * N : (b + 1) * N],
+                start=True,
+                stop=True,
+            )
+            scores.append(acc)
+        for b in range(B):
+            result = sb.tile([P, N], F32, name="result%d" % b)
+            nc.vector.tensor_tensor(result[:], scores[b][:], bias[b][:], ADD)
+            nc.sync.dma_start(out[b], result[:])

@@ -27,72 +27,86 @@ def tile_attend_lq_score_kernel(tc, qT, k_words, k_scales, kb, offq, offs, out):
 
         key_list = sb.tile([P, B * N // 16], U16, name="key_list")
         query_list = sb.tile([P, B * NQ // 16], U16, name="query_list")
-        q_planes = [sb.tile([P, TQ], F32, name="q_plane%d" % t) for t in range(PACK)]
+        q_halves = [sb.tile([P, 2, TQ // 2], F32, name="q_half%d" % h) for h in range(2)]
+        q_planes = [sb.tile([P, TQ], F32, name="q_plane%d" % t) for t in (2, 3)]
         word_pool = sb.tile([P, T], I32, name="word_pool")
-        scale_pool = sb.tile([P, T // 4], I32, name="scale_pool")
+        scale_pool = sb.tile([P, T // 4], I32, name="scale_pool", tag="early", align_bytes=64)
         bias_pool = sb.tile([P, T], F32, name="bias_pool")
         ident = sb.tile([P, P], F32, name="ident")
 
-        nc.vector.memset(scale_pool[:], 0)
+        nc.gpsimd.memset(scale_pool[:], 0)
         nc.vector.memset(bias_pool[0 : P - 1, :], 0.0)
         make_identity(nc, ident[:])
 
         q_rows = qT.rearrange("(p t) n -> p t n", t=PACK)
         nc.sync.dma_start(key_list[:], offs)
         nc.scalar.dma_start(bias_pool[P - 1 : P, :], kb[0:1, :])
-        nc.sync.dma_start(q_planes[0][:], q_rows[:, 0, :])
         nc.sync.dma_start(query_list[:], offq)
-        for t in range(1, PACK):
-            nc.sync.dma_start(q_planes[t][:], q_rows[:, t, :])
-        nc.sync.dma_start(word_pool[:], k_words[0].rearrange("p t r -> p (t r)").bitcast(I32))
+        nc.sync.dma_start(q_halves[0][:], q_rows[:, 0:2, 0 : TQ // 2])
         for quad in range(4):
-            nc.scalar.dma_start(
+            nc.sync.dma_start(
                 scale_pool[32 * quad : 32 * quad + 4, :], k_scales[0, 4 * quad : 4 * quad + 4, :].bitcast(I32)
             )
+        nc.sync.dma_start(q_halves[1][:], q_rows[:, 0:2, TQ // 2 : TQ])
+        for t in range(2):
+            nc.sync.dma_start(q_planes[t][:], q_rows[:, 2 + t, :])
+        nc.sync.dma_start(word_pool[:], k_words[0].rearrange("p t r -> p (t r)").bitcast(I32))
+
+        q_pairs = sb.tile([P, TQ, 2], BF16, name="q_pairs")
+        for h in range(2):
+            nc.scalar.copy(q_pairs[:, h * TQ // 2 : (h + 1) * TQ // 2, :], q_halves[h][:].rearrange("p t n -> p n t"))
 
         bias_row = sb.tile([P, B * N], F32, name="bias_row")
         nc.vector.tensor_copy(bias_row[:], bias_pool[:].indirect(key_list[:]))
+        key_scales = sb.tile([P, B * N], U8, name="key_scales", align_bytes=64)
+        nc.vector.tensor_copy(key_scales[:], scale_pool[:].bitcast(U8).indirect(key_list[:]))
+
         bias_col = sb.tile([P, B * N // P], F32, name="bias_col")
         for b in range(B):
-            turned = ps.tile([P, 4, P], F32, name="turned%d" % b)
+            turned = ps.tile([P, 4, P], F32, name="turned%d" % b, tag="bank%d" % (2 + b))
             for c in range(4):
                 nc.tensor.transpose(turned[:, c, :], bias_row[:, b * N + c * P : b * N + (c + 1) * P], ident[:])
             nc.scalar.copy(bias_col[:, 4 * b : 4 * b + 4], turned[:, :, P - 1])
         bias = []
         for b in range(B):
-            spread = ps.tile([P, 4, P], F32, name="spread%d" % b)
+            spread = ps.tile([P, 4, P], F32, name="spread%d" % b, tag="bank%d" % (1 - b))
             for c in range(4):
                 nc.tensor.transpose(spread[:, c, :], bias_col[:, 4 * b + c : 4 * b + c + 1].to_broadcast([P, P]), ident[:])
             bias_b = sb.tile([P, N], F32, name="bias%d" % b)
             nc.scalar.copy(bias_b[:], spread[:].rearrange("p c n -> p (c n)"))
             bias.append(bias_b)
 
-        q_grouped = sb.tile([P, B * NQ, PACK], BF16, name="q_grouped", align_bytes=64)
-        key_scales = sb.tile([P, B * N], U8, name="key_scales", align_bytes=64)
-        nc.vector.tensor_copy(q_grouped[:, :, 0], q_planes[0][:].indirect(query_list[:]))
-        nc.vector.tensor_copy(key_scales[:], scale_pool[:].bitcast(U8).indirect(key_list[:]))
-        for t in range(1, PACK):
-            nc.vector.tensor_copy(q_grouped[:, :, t], q_planes[t][:].indirect(query_list[:]))
+        q_grouped = sb.tile([P, B * NQ, PACK], BF16, name="q_grouped", tag="early", align_bytes=64)
+        nc.vector.tensor_copy(
+            q_grouped[:].bitcast(U32)[:, :, 0],
+            q_pairs[:].rearrange("p n t -> p (n t)").bitcast(U32).indirect(query_list[:]),
+        )
+        for t in range(2):
+            nc.vector.tensor_copy(q_grouped[:, :, 2 + t], q_planes[t][:].indirect(query_list[:]))
         q_codes = sb.tile([P, B * NQ], U32, name="q_codes", align_bytes=64)
         q_scales = sb.tile([P, B * NQ], U8, name="q_scales", align_bytes=64)
         nc.vector.quantize_mx(out=q_codes[:].bitcast(FP8X4), scales=q_scales[:], in_=q_grouped[:].rearrange("p n t -> p (n t)"))
 
+        H = N // 2
         scores = []
         for b in range(B):
             key_words = sb.tile([P, N], U32, name="key_words%d" % b, align_bytes=64)
             nc.vector.tensor_copy(key_words[:], word_pool[:].bitcast(U32).indirect(key_list[:, b * N // 16 : (b + 1) * N // 16]))
-            acc = ps.tile([P, N], F32, name="scores%d" % b)
-            nc.tensor.matmul_mx(
-                out=acc[:],
-                lhsT=q_codes[:, b * NQ : (b + 1) * NQ].bitcast(FP8X4),
-                lhsT_scale=q_scales[:, b * NQ : (b + 1) * NQ],
-                rhs=key_words[:].bitcast(FP8X4),
-                rhs_scale=key_scales[:, b * N : (b + 1) * N],
-                start=True,
-                stop=True,
-            )
-            scores.append(acc)
+            for h in range(2):
+                acc = ps.tile([P, H], F32, name="scores%d" % (2 * b + h), tag="bank%d" % (2 * b + h))
+                nc.tensor.matmul_mx(
+                    out=acc[:],
+                    lhsT=q_codes[:, b * NQ : (b + 1) * NQ].bitcast(FP8X4),
+                    lhsT_scale=q_scales[:, b * NQ : (b + 1) * NQ],
+                    rhs=key_words[:, h * H : (h + 1) * H].bitcast(FP8X4),
+                    rhs_scale=key_scales[:, b * N + h * H : b * N + (h + 1) * H],
+                    start=True,
+                    stop=True,
+                )
+                scores.append(acc)
         for b in range(B):
-            result = sb.tile([P, N], F32, name="result%d" % b)
-            nc.vector.tensor_tensor(result[:], scores[b][:], bias[b][:], ADD)
-            nc.sync.dma_start(out[b], result[:])
+            for h in range(2):
+                result = sb.tile([P, H], F32, name="result%d" % (2 * b + h))
+                nc.vector.tensor_tensor(result[:], scores[2 * b + h][:], bias[b][:, h * H : (h + 1) * H], ADD)
+                queue = nc.sync if h == 0 else nc.scalar
+                queue.dma_start(out[b, :, h * H : (h + 1) * H], result[:])

@@ -42,11 +42,9 @@ def tile_attend_lq_score_kernel(tc, qT, k_words, k_scales, kb, offq, offs, out):
         nc.sync.dma_start(key_list[:], offs)
         nc.scalar.dma_start(bias_pool[P - 1 : P, :], kb[0:1, :])
         nc.sync.dma_start(query_list[:], offq)
-        nc.sync.dma_start(q_halves[0][:], q_rows[:, 0:2, 0 : TQ // 2])
+        nc.scalar.dma_start(q_halves[0][:], q_rows[:, 0:2, 0 : TQ // 2])
         for quad in range(4):
-            nc.sync.dma_start(
-                scale_pool[32 * quad : 32 * quad + 4, :], k_scales[0, 4 * quad : 4 * quad + 4, :].bitcast(I32)
-            )
+            nc.sync.dma_start(scale_pool[28 * quad : 28 * quad + 16, :], k_scales[0].bitcast(I32))
         nc.sync.dma_start(q_halves[1][:], q_rows[:, 0:2, TQ // 2 : TQ])
         for t in range(2):
             nc.sync.dma_start(q_planes[t][:], q_rows[:, 2 + t, :])

@@ -17,6 +17,7 @@ U16 = mybir.dt.uint16
 U8 = mybir.dt.uint8
 FP8X4 = mybir.dt.float8_e4m3fn_x4
 ADD = mybir.AluOpType.add
+COPY = mybir.ActivationFunctionType.Copy
 
 
 def tile_attend_lq_score_kernel(tc, qT, k_words, k_scales, kb, offq, offs, out):
@@ -27,10 +28,10 @@ def tile_attend_lq_score_kernel(tc, qT, k_words, k_scales, kb, offq, offs, out):
 
         key_list = sb.tile([P, B * N // 16], U16, name="key_list")
         query_list = sb.tile([P, B * NQ // 16], U16, name="query_list")
-        q_halves = [sb.tile([P, 2, TQ // 2], F32, name="q_half%d" % h) for h in range(2)]
-        q_planes = [sb.tile([P, TQ], F32, name="q_plane%d" % t) for t in (2, 3)]
+        q_front = [sb.tile([P, TQ], F32, name="q_plane%d" % t) for t in range(2)]
+        q_back = sb.tile([P, 2, TQ], F32, name="q_back")
         word_pool = sb.tile([P, T], I32, name="word_pool")
-        scale_pool = sb.tile([P, T // 4], I32, name="scale_pool", tag="early", align_bytes=64)
+        scale_pool = sb.tile([P, T // 4], I32, name="scale_pool", align_bytes=64)
         bias_pool = sb.tile([P, T], F32, name="bias_pool")
         ident = sb.tile([P, P], F32, name="ident")
 
@@ -39,51 +40,47 @@ def tile_attend_lq_score_kernel(tc, qT, k_words, k_scales, kb, offq, offs, out):
         make_identity(nc, ident[:])
 
         q_rows = qT.rearrange("(p t) n -> p t n", t=PACK)
+        scale_rows = k_scales[0].bitcast(I32).rearrange("(quad r) n -> r quad n", r=4)
         nc.sync.dma_start(key_list[:], offs)
         nc.scalar.dma_start(bias_pool[P - 1 : P, :], kb[0:1, :])
-        nc.sync.dma_start(query_list[:], offq)
-        nc.scalar.dma_start(q_halves[0][:], q_rows[:, 0:2, 0 : TQ // 2])
-        for quad in range(4):
-            nc.sync.dma_start(scale_pool[28 * quad : 28 * quad + 16, :], k_scales[0].bitcast(I32))
-        nc.sync.dma_start(q_halves[1][:], q_rows[:, 0:2, TQ // 2 : TQ])
         for t in range(2):
-            nc.sync.dma_start(q_planes[t][:], q_rows[:, 2 + t, :])
+            nc.scalar.dma_start(q_front[t][:], q_rows[:, t, :])
+        for r in range(4):
+            nc.sync.dma_start(scale_pool[r:P:32, :], scale_rows[r])
+        nc.sync.dma_start(query_list[:], offq)
+        nc.sync.dma_start(q_back[:], q_rows[:, 2:4, :])
         nc.sync.dma_start(word_pool[:], k_words[0].rearrange("p t r -> p (t r)").bitcast(I32))
-
-        q_pairs = sb.tile([P, TQ, 2], BF16, name="q_pairs")
-        for h in range(2):
-            nc.scalar.copy(q_pairs[:, h * TQ // 2 : (h + 1) * TQ // 2, :], q_halves[h][:].rearrange("p t n -> p n t"))
 
         bias_row = sb.tile([P, B * N], F32, name="bias_row")
         nc.vector.tensor_copy(bias_row[:], bias_pool[:].indirect(key_list[:]))
         key_scales = sb.tile([P, B * N], U8, name="key_scales", align_bytes=64)
         nc.vector.tensor_copy(key_scales[:], scale_pool[:].bitcast(U8).indirect(key_list[:]))
 
-        bias_col = sb.tile([P, B * N // P], F32, name="bias_col")
+        q_grouped = sb.tile([P, B * NQ, PACK], BF16, name="q_grouped", align_bytes=64)
+        for t in range(2):
+            q_round = sb.tile([P, TQ], BF16, name="q_round%d" % t, tag="round%d" % t)
+            nc.scalar.copy(q_round[:], q_front[t][:])
+            nc.scalar.activation(q_grouped[:, :, t], q_round[:].indirect(query_list[:]), COPY)
+        for t in range(2):
+            nc.vector.tensor_copy(q_grouped[:, :, 2 + t], q_back[:, t, :].indirect(query_list[:]))
+        q_codes = sb.tile([P, B * NQ], U32, name="q_codes", align_bytes=64)
+        q_scales = sb.tile([P, B * NQ], U8, name="q_scales", align_bytes=64)
+        nc.vector.quantize_mx(out=q_codes[:].bitcast(FP8X4), scales=q_scales[:], in_=q_grouped[:].rearrange("p n t -> p (n t)"))
+
+        bias_col = sb.tile([P, B * N // P], F32, name="bias_col", tag="round1")
         for b in range(B):
-            turned = ps.tile([P, 4, P], F32, name="turned%d" % b, tag="bank%d" % (2 + b))
+            turned = ps.tile([P, 4, P], F32, name="turned%d" % b)
             for c in range(4):
                 nc.tensor.transpose(turned[:, c, :], bias_row[:, b * N + c * P : b * N + (c + 1) * P], ident[:])
             nc.scalar.copy(bias_col[:, 4 * b : 4 * b + 4], turned[:, :, P - 1])
         bias = []
         for b in range(B):
-            spread = ps.tile([P, 4, P], F32, name="spread%d" % b, tag="bank%d" % (1 - b))
+            spread = ps.tile([P, 4, P], F32, name="spread%d" % b)
             for c in range(4):
                 nc.tensor.transpose(spread[:, c, :], bias_col[:, 4 * b + c : 4 * b + c + 1].to_broadcast([P, P]), ident[:])
             bias_b = sb.tile([P, N], F32, name="bias%d" % b)
             nc.scalar.copy(bias_b[:], spread[:].rearrange("p c n -> p (c n)"))
             bias.append(bias_b)
-
-        q_grouped = sb.tile([P, B * NQ, PACK], BF16, name="q_grouped", tag="early", align_bytes=64)
-        nc.vector.tensor_copy(
-            q_grouped[:].bitcast(U32)[:, :, 0],
-            q_pairs[:].rearrange("p n t -> p (n t)").bitcast(U32).indirect(query_list[:]),
-        )
-        for t in range(2):
-            nc.vector.tensor_copy(q_grouped[:, :, 2 + t], q_planes[t][:].indirect(query_list[:]))
-        q_codes = sb.tile([P, B * NQ], U32, name="q_codes", align_bytes=64)
-        q_scales = sb.tile([P, B * NQ], U8, name="q_scales", align_bytes=64)
-        nc.vector.quantize_mx(out=q_codes[:].bitcast(FP8X4), scales=q_scales[:], in_=q_grouped[:].rearrange("p n t -> p (n t)"))
 
         H = N // 2
         scores = []
@@ -91,7 +88,7 @@ def tile_attend_lq_score_kernel(tc, qT, k_words, k_scales, kb, offq, offs, out):
             key_words = sb.tile([P, N], U32, name="key_words%d" % b, align_bytes=64)
             nc.vector.tensor_copy(key_words[:], word_pool[:].bitcast(U32).indirect(key_list[:, b * N // 16 : (b + 1) * N // 16]))
             for h in range(2):
-                acc = ps.tile([P, H], F32, name="scores%d" % (2 * b + h), tag="bank%d" % (2 * b + h))
+                acc = ps.tile([P, H], F32, name="scores%d" % (2 * b + h))
                 nc.tensor.matmul_mx(
                     out=acc[:],
                     lhsT=q_codes[:, b * NQ : (b + 1) * NQ].bitcast(FP8X4),

@@ -28,7 +28,7 @@ def tile_attend_lq_score_kernel(tc, qT, k_words, k_scales, kb, offq, offs, out):
 
         key_list = sb.tile([P, B * N // 16], U16, name="key_list")
         query_list = sb.tile([P, B * NQ // 16], U16, name="query_list")
-        q_front = [sb.tile([P, TQ], F32, name="q_plane%d" % t) for t in range(2)]
+        q_front = sb.tile([P, 2, TQ], F32, name="q_front")
         q_back = sb.tile([P, 2, TQ], F32, name="q_back")
         word_pool = sb.tile([P, T], I32, name="word_pool")
         scale_pool = sb.tile([P, T // 4], I32, name="scale_pool", align_bytes=64)
@@ -42,12 +42,11 @@ def tile_attend_lq_score_kernel(tc, qT, k_words, k_scales, kb, offq, offs, out):
         q_rows = qT.rearrange("(p t) n -> p t n", t=PACK)
         scale_rows = k_scales[0].bitcast(I32).rearrange("(quad r) n -> r quad n", r=4)
         nc.sync.dma_start(key_list[:], offs)
-        nc.scalar.dma_start(bias_pool[P - 1 : P, :], kb[0:1, :])
-        for t in range(2):
-            nc.scalar.dma_start(q_front[t][:], q_rows[:, t, :])
+        nc.sync.dma_start(bias_pool[P - 1 : P, :], kb[0:1, :])
+        nc.sync.dma_start(q_front[:], q_rows[:, 0:2, :])
+        nc.sync.dma_start(query_list[:], offq)
         for r in range(4):
             nc.sync.dma_start(scale_pool[r:P:32, :], scale_rows[r])
-        nc.sync.dma_start(query_list[:], offq)
         nc.sync.dma_start(q_back[:], q_rows[:, 2:4, :])
         nc.sync.dma_start(word_pool[:], k_words[0].rearrange("p t r -> p (t r)").bitcast(I32))
 
@@ -59,7 +58,7 @@ def tile_attend_lq_score_kernel(tc, qT, k_words, k_scales, kb, offq, offs, out):
         q_grouped = sb.tile([P, B * NQ, PACK], BF16, name="q_grouped", align_bytes=64)
         for t in range(2):
             q_round = sb.tile([P, TQ], BF16, name="q_round%d" % t, tag="round%d" % t)
-            nc.scalar.copy(q_round[:], q_front[t][:])
+            nc.scalar.copy(q_round[:], q_front[:, t, :])
             nc.scalar.activation(q_grouped[:, :, t], q_round[:].indirect(query_list[:]), COPY)
         for t in range(2):
             nc.vector.tensor_copy(q_grouped[:, :, 2 + t], q_back[:, t, :].indirect(query_list[:]))

@@ -17,7 +17,6 @@ U16 = mybir.dt.uint16
 U8 = mybir.dt.uint8
 FP8X4 = mybir.dt.float8_e4m3fn_x4
 ADD = mybir.AluOpType.add
-COPY = mybir.ActivationFunctionType.Copy
 
 
 def tile_attend_lq_score_kernel(tc, qT, k_words, k_scales, kb, offq, offs, out):
@@ -29,7 +28,7 @@ def tile_attend_lq_score_kernel(tc, qT, k_words, k_scales, kb, offq, offs, out):
         key_list = sb.tile([P, B * N // 16], U16, name="key_list")
         query_list = sb.tile([P, B * NQ // 16], U16, name="query_list")
         q_front = sb.tile([P, 2, TQ], F32, name="q_front")
-        q_back = sb.tile([P, 2, TQ], F32, name="q_back")
+        q_back = [sb.tile([P, TQ], F32, name="q_plane%d" % t) for t in (2, 3)]
         word_pool = sb.tile([P, T], I32, name="word_pool")
         scale_pool = sb.tile([P, T // 4], I32, name="scale_pool", align_bytes=64)
         bias_pool = sb.tile([P, T], F32, name="bias_pool")
@@ -47,26 +46,30 @@ def tile_attend_lq_score_kernel(tc, qT, k_words, k_scales, kb, offq, offs, out):
         nc.sync.dma_start(query_list[:], offq)
         for r in range(4):
             nc.sync.dma_start(scale_pool[r:P:32, :], scale_rows[r])
-        nc.sync.dma_start(q_back[:], q_rows[:, 2:4, :])
+        for t in range(2):
+            nc.sync.dma_start(q_back[t][:], q_rows[:, 2 + t, :])
         nc.sync.dma_start(word_pool[:], k_words[0].rearrange("p t r -> p (t r)").bitcast(I32))
 
         bias_row = sb.tile([P, B * N], F32, name="bias_row")
         nc.vector.tensor_copy(bias_row[:], bias_pool[:].indirect(key_list[:]))
+        q_picked = sb.tile([P, PACK, B * NQ], F32, name="q_picked")
+        for t in range(2):
+            nc.vector.tensor_copy(q_picked[:, t, :], q_front[:, t, :].indirect(query_list[:]))
         key_scales = sb.tile([P, B * N], U8, name="key_scales", align_bytes=64)
         nc.vector.tensor_copy(key_scales[:], scale_pool[:].bitcast(U8).indirect(key_list[:]))
+        for t in range(2):
+            nc.vector.tensor_copy(q_picked[:, 2 + t, :], q_back[t][:].indirect(query_list[:]))
 
         q_grouped = sb.tile([P, B * NQ, PACK], BF16, name="q_grouped", align_bytes=64)
-        for t in range(2):
-            q_round = sb.tile([P, TQ], BF16, name="q_round%d" % t, tag="round%d" % t)
-            nc.scalar.copy(q_round[:], q_front[:, t, :])
-            nc.scalar.activation(q_grouped[:, :, t], q_round[:].indirect(query_list[:]), COPY)
-        for t in range(2):
-            nc.vector.tensor_copy(q_grouped[:, :, 2 + t], q_back[:, t, :].indirect(query_list[:]))
+        nc.vector.tensor_copy(
+            q_grouped[:].rearrange("p (c i) t -> p c t i", i=4),
+            q_picked[:].rearrange("p t (c i) -> p c t i", i=4),
+        )
         q_codes = sb.tile([P, B * NQ], U32, name="q_codes", align_bytes=64)
         q_scales = sb.tile([P, B * NQ], U8, name="q_scales", align_bytes=64)
         nc.vector.quantize_mx(out=q_codes[:].bitcast(FP8X4), scales=q_scales[:], in_=q_grouped[:].rearrange("p n t -> p (n t)"))
 
-        bias_col = sb.tile([P, B * N // P], F32, name="bias_col", tag="round1")
+        bias_col = sb.tile([P, B * N // P], F32, name="bias_col")
         for b in range(B):
             turned = ps.tile([P, 4, P], F32, name="turned%d" % b)
             for c in range(4):

@@ -34,7 +34,7 @@ def tile_attend_lq_score_kernel(tc, qT, k_words, k_scales, kb, offq, offs, out):
         bias_pool = sb.tile([P, T], F32, name="bias_pool")
         ident = sb.tile([P, P], F32, name="ident")
 
-        nc.gpsimd.memset(scale_pool[:], 0)
+        nc.vector.memset(scale_pool[:], 0)
         nc.vector.memset(bias_pool[0 : P - 1, :], 0.0)
         make_identity(nc, ident[:])
 
@@ -42,32 +42,43 @@ def tile_attend_lq_score_kernel(tc, qT, k_words, k_scales, kb, offq, offs, out):
         scale_rows = k_scales[0].bitcast(I32).rearrange("(quad r) n -> r quad n", r=4)
         nc.sync.dma_start(key_list[:], offs)
         nc.sync.dma_start(bias_pool[P - 1 : P, :], kb[0:1, :])
+        for r in range(4):
+            queue = nc.sync if r < 2 else nc.scalar
+            queue.dma_start(scale_pool[r:P:32, :], scale_rows[r])
         nc.sync.dma_start(q_front[:], q_rows[:, 0:2, :])
         nc.sync.dma_start(query_list[:], offq)
-        for r in range(4):
-            nc.sync.dma_start(scale_pool[r:P:32, :], scale_rows[r])
         for t in range(2):
             nc.sync.dma_start(q_back[t][:], q_rows[:, 2 + t, :])
         nc.sync.dma_start(word_pool[:], k_words[0].rearrange("p t r -> p (t r)").bitcast(I32))
 
         bias_row = sb.tile([P, B * N], F32, name="bias_row")
         nc.vector.tensor_copy(bias_row[:], bias_pool[:].indirect(key_list[:]))
+        key_scales = sb.tile([P, B * N], U8, name="key_scales", align_bytes=64)
+        nc.vector.tensor_copy(key_scales[:], scale_pool[:].bitcast(U8).indirect(key_list[:]))
         q_picked = sb.tile([P, PACK, B * NQ], F32, name="q_picked")
         for t in range(2):
             nc.vector.tensor_copy(q_picked[:, t, :], q_front[:, t, :].indirect(query_list[:]))
-        key_scales = sb.tile([P, B * N], U8, name="key_scales", align_bytes=64)
-        nc.vector.tensor_copy(key_scales[:], scale_pool[:].bitcast(U8).indirect(key_list[:]))
-        for t in range(2):
-            nc.vector.tensor_copy(q_picked[:, 2 + t, :], q_back[t][:].indirect(query_list[:]))
+        nc.vector.tensor_copy(q_picked[:, 2, :], q_back[0][:].indirect(query_list[:]))
+        for b in range(B):
+            nc.vector.tensor_copy(
+                q_picked[:, 3, b * NQ : (b + 1) * NQ],
+                q_back[1][:].indirect(query_list[:, b * NQ // 16 : (b + 1) * NQ // 16]),
+            )
 
         q_grouped = sb.tile([P, B * NQ, PACK], BF16, name="q_grouped", align_bytes=64)
-        nc.vector.tensor_copy(
-            q_grouped[:].rearrange("p (c i) t -> p c t i", i=4),
-            q_picked[:].rearrange("p t (c i) -> p c t i", i=4),
-        )
+        for b in range(B):
+            nc.vector.tensor_copy(
+                q_grouped[:, b * NQ : (b + 1) * NQ, :].rearrange("p (c i) t -> p c t i", i=4),
+                q_picked[:, :, b * NQ : (b + 1) * NQ].rearrange("p t (c i) -> p c t i", i=4),
+            )
         q_codes = sb.tile([P, B * NQ], U32, name="q_codes", align_bytes=64)
         q_scales = sb.tile([P, B * NQ], U8, name="q_scales", align_bytes=64)
-        nc.vector.quantize_mx(out=q_codes[:].bitcast(FP8X4), scales=q_scales[:], in_=q_grouped[:].rearrange("p n t -> p (n t)"))
+        for b in range(B):
+            nc.vector.quantize_mx(
+                out=q_codes[:, b * NQ : (b + 1) * NQ].bitcast(FP8X4),
+                scales=q_scales[:, b * NQ : (b + 1) * NQ],
+                in_=q_grouped[:, b * NQ : (b + 1) * NQ, :].rearrange("p n t -> p (n t)"),
+            )
 
         bias_col = sb.tile([P, B * N // P], F32, name="bias_col")
         for b in range(B):

@@ -82,7 +82,7 @@ def tile_attend_lq_score_kernel(tc, qT, k_words, k_scales, kb, offq, offs, out):
 
         bias_col = sb.tile([P, B * N // P], F32, name="bias_col")
         for b in range(B):
-            turned = ps.tile([P, 4, P], F32, name="turned%d" % b)
+            turned = ps.tile([P, 4, P], F32, name="turned%d" % b, tag="turned%d" % b)
             for c in range(4):
                 nc.tensor.transpose(turned[:, c, :], bias_row[:, b * N + c * P : b * N + (c + 1) * P], ident[:])
             nc.scalar.copy(bias_col[:, 4 * b : 4 * b + 4], turned[:, :, P - 1])
@@ -96,25 +96,29 @@ def tile_attend_lq_score_kernel(tc, qT, k_words, k_scales, kb, offq, offs, out):
             bias.append(bias_b)
 
         H = N // 2
-        scores = []
-        for b in range(B):
-            key_words = sb.tile([P, N], U32, name="key_words%d" % b, align_bytes=64)
-            nc.vector.tensor_copy(key_words[:], word_pool[:].bitcast(U32).indirect(key_list[:, b * N // 16 : (b + 1) * N // 16]))
-            for h in range(2):
-                acc = ps.tile([P, H], F32, name="scores%d" % (2 * b + h))
+        pieces = []
+        for g in range(2 * B):
+            b, lo = g // 2, g % 2 * H
+            key_words = sb.tile([P, H], U32, name="key_words%d" % g, align_bytes=64)
+            nc.vector.tensor_copy(
+                key_words[:], word_pool[:].bitcast(U32).indirect(key_list[:, g * H // 16 : (g + 1) * H // 16])
+            )
+            width = H // 2 if g == 2 * B - 1 else H
+            for c in range(0, H, width):
+                i = len(pieces)
+                acc = ps.tile([P, width], F32, name="scores%d" % i, tag="turned0" if i == 4 else "scores%d" % i)
                 nc.tensor.matmul_mx(
                     out=acc[:],
                     lhsT=q_codes[:, b * NQ : (b + 1) * NQ].bitcast(FP8X4),
                     lhsT_scale=q_scales[:, b * NQ : (b + 1) * NQ],
-                    rhs=key_words[:, h * H : (h + 1) * H].bitcast(FP8X4),
-                    rhs_scale=key_scales[:, b * N + h * H : b * N + (h + 1) * H],
+                    rhs=key_words[:, c : c + width].bitcast(FP8X4),
+                    rhs_scale=key_scales[:, b * N + lo + c : b * N + lo + c + width],
                     start=True,
                     stop=True,
                 )
-                scores.append(acc)
-        for b in range(B):
-            for h in range(2):
-                result = sb.tile([P, H], F32, name="result%d" % (2 * b + h))
-                nc.vector.tensor_tensor(result[:], scores[2 * b + h][:], bias[b][:, h * H : (h + 1) * H], ADD)
-                queue = nc.sync if h == 0 else nc.scalar
-                queue.dma_start(out[b, :, h * H : (h + 1) * H], result[:])
+                pieces.append((b, slice(lo + c, lo + c + width), acc))
+        for i, (b, cols, acc) in enumerate(pieces):
+            result = sb.tile([P, cols.stop - cols.start], F32, name="result%d" % i)
+            nc.vector.tensor_tensor(result[:], acc[:], bias[b][:, cols], ADD)
+            queue = nc.sync if i % 2 == 0 else nc.scalar
+            queue.dma_start(out[b, :, cols], result[:])

@@ -65,10 +65,11 @@ def tile_attend_lq_score_kernel(tc, qT, k_words, k_scales, kb, offq, offs, out):
                 q_back[1][:].indirect(query_list[:, b * NQ // 16 : (b + 1) * NQ // 16]),
             )
 
-        q_grouped = sb.tile([P, B * NQ, PACK], BF16, name="q_grouped", align_bytes=64)
+        q_grouped = [sb.tile([P, NQ, PACK], BF16, name="q_grouped%d" % b, align_bytes=64) for b in range(B)]
         for b in range(B):
-            nc.vector.tensor_copy(
-                q_grouped[:, b * NQ : (b + 1) * NQ, :].rearrange("p (c i) t -> p c t i", i=4),
+            weave = nc.scalar.copy if b == 0 else nc.vector.tensor_copy
+            weave(
+                q_grouped[b][:].rearrange("p (c i) t -> p c t i", i=4),
                 q_picked[:, :, b * NQ : (b + 1) * NQ].rearrange("p t (c i) -> p c t i", i=4),
             )
         q_codes = sb.tile([P, B * NQ], U32, name="q_codes", align_bytes=64)
@@ -77,7 +78,7 @@ def tile_attend_lq_score_kernel(tc, qT, k_words, k_scales, kb, offq, offs, out):
             nc.vector.quantize_mx(
                 out=q_codes[:, b * NQ : (b + 1) * NQ].bitcast(FP8X4),
                 scales=q_scales[:, b * NQ : (b + 1) * NQ],
-                in_=q_grouped[:, b * NQ : (b + 1) * NQ, :].rearrange("p n t -> p (n t)"),
+                in_=q_grouped[b][:].rearrange("p n t -> p (n t)"),
             )
 
         bias_col = sb.tile([P, B * N // P], F32, name="bias_col")

@@ -27,42 +27,42 @@ def tile_attend_lq_score_kernel(tc, qT, k_words, k_scales, kb, offq, offs, out):
 
         key_list = sb.tile([P, B * N // 16], U16, name="key_list")
         query_list = sb.tile([P, B * NQ // 16], U16, name="query_list")
-        q_front = sb.tile([P, 2, TQ], F32, name="q_front")
-        q_back = [sb.tile([P, TQ], F32, name="q_plane%d" % t) for t in (2, 3)]
+        q_front = sb.tile([P, 3 * TQ], F32, name="q_front")
+        q_last = sb.tile([P, TQ], F32, name="q_last")
         word_pool = sb.tile([P, T], I32, name="word_pool")
         scale_pool = sb.tile([P, T // 4], I32, name="scale_pool", align_bytes=64)
-        bias_pool = sb.tile([P, T], F32, name="bias_pool")
+        bias_pool = sb.tile([P, T], F32, name="bias_pool", tag="bias_then_scales", align_bytes=64)
         ident = sb.tile([P, P], F32, name="ident")
 
         nc.vector.memset(scale_pool[:], 0)
         nc.vector.memset(bias_pool[0 : P - 1, :], 0.0)
         make_identity(nc, ident[:])
 
-        q_rows = qT.rearrange("(p t) n -> p t n", t=PACK)
+        q_rows = qT.rearrange("(p t) n -> p (t n)", t=PACK)
+        HEAD = TQ // 2
         scale_rows = k_scales[0].bitcast(I32).rearrange("(quad r) n -> r quad n", r=4)
         nc.sync.dma_start(key_list[:], offs)
-        nc.sync.dma_start(bias_pool[P - 1 : P, :], kb[0:1, :])
+        nc.sync.dma_start(q_front[:, 0:HEAD], q_rows[:, 0:HEAD])
         for r in range(4):
             queue = nc.sync if r < 2 else nc.scalar
             queue.dma_start(scale_pool[r:P:32, :], scale_rows[r])
-        nc.sync.dma_start(q_front[:], q_rows[:, 0:2, :])
+        nc.sync.dma_start(bias_pool[P - 1 : P, :], kb[0:1, :])
+        nc.sync.dma_start(q_front[:, HEAD:], q_rows[:, HEAD : 3 * TQ])
         nc.sync.dma_start(query_list[:], offq)
-        for t in range(2):
-            nc.sync.dma_start(q_back[t][:], q_rows[:, 2 + t, :])
+        nc.sync.dma_start(q_last[:], q_rows[:, 3 * TQ :])
         nc.sync.dma_start(word_pool[:], k_words[0].rearrange("p t r -> p (t r)").bitcast(I32))
 
         bias_row = sb.tile([P, B * N], F32, name="bias_row")
         nc.vector.tensor_copy(bias_row[:], bias_pool[:].indirect(key_list[:]))
-        key_scales = sb.tile([P, B * N], U8, name="key_scales", align_bytes=64)
+        key_scales = sb.tile([P, B * N], U8, name="key_scales", tag="bias_then_scales", align_bytes=64)
         nc.vector.tensor_copy(key_scales[:], scale_pool[:].bitcast(U8).indirect(key_list[:]))
         q_picked = sb.tile([P, PACK, B * NQ], F32, name="q_picked")
-        for t in range(2):
-            nc.vector.tensor_copy(q_picked[:, t, :], q_front[:, t, :].indirect(query_list[:]))
-        nc.vector.tensor_copy(q_picked[:, 2, :], q_back[0][:].indirect(query_list[:]))
+        for t in range(3):
+            nc.vector.tensor_copy(q_picked[:, t, :], q_front[:, t * TQ : (t + 1) * TQ].indirect(query_list[:]))
         for b in range(B):
             nc.vector.tensor_copy(
                 q_picked[:, 3, b * NQ : (b + 1) * NQ],
-                q_back[1][:].indirect(query_list[:, b * NQ // 16 : (b + 1) * NQ // 16]),
+                q_last[:].indirect(query_list[:, b * NQ // 16 : (b + 1) * NQ // 16]),
             )
 
         q_grouped = [sb.tile([P, NQ, PACK], BF16, name="q_grouped%d" % b, align_bytes=64) for b in range(B)]

@@ -31,7 +31,7 @@ def tile_attend_lq_score_kernel(tc, qT, k_words, k_scales, kb, offq, offs, out):
         q_last = sb.tile([P, TQ], F32, name="q_last")
         word_pool = sb.tile([P, T], I32, name="word_pool")
         scale_pool = sb.tile([P, T // 4], I32, name="scale_pool", align_bytes=64)
-        bias_pool = sb.tile([P, T], F32, name="bias_pool", tag="bias_then_scales", align_bytes=64)
+        bias_pool = sb.tile([P, T], F32, name="bias_pool")
         ident = sb.tile([P, P], F32, name="ident")
 
         nc.vector.memset(scale_pool[:], 0)
@@ -47,16 +47,17 @@ def tile_attend_lq_score_kernel(tc, qT, k_words, k_scales, kb, offq, offs, out):
             queue = nc.sync if r < 2 else nc.scalar
             queue.dma_start(scale_pool[r:P:32, :], scale_rows[r])
         nc.sync.dma_start(bias_pool[P - 1 : P, :], kb[0:1, :])
-        nc.sync.dma_start(q_front[:, HEAD:], q_rows[:, HEAD : 3 * TQ])
+        nc.sync.dma_start(q_front[:, HEAD : HEAD + 2 * TQ], q_rows[:, HEAD : HEAD + 2 * TQ])
         nc.sync.dma_start(query_list[:], offq)
+        nc.sync.dma_start(q_front[:, HEAD + 2 * TQ :], q_rows[:, HEAD + 2 * TQ : 3 * TQ])
         nc.sync.dma_start(q_last[:], q_rows[:, 3 * TQ :])
         nc.sync.dma_start(word_pool[:], k_words[0].rearrange("p t r -> p (t r)").bitcast(I32))
 
         bias_row = sb.tile([P, B * N], F32, name="bias_row")
         nc.vector.tensor_copy(bias_row[:], bias_pool[:].indirect(key_list[:]))
-        key_scales = sb.tile([P, B * N], U8, name="key_scales", tag="bias_then_scales", align_bytes=64)
+        key_scales = sb.tile([P, B * N], U8, name="key_scales", align_bytes=64)
         nc.vector.tensor_copy(key_scales[:], scale_pool[:].bitcast(U8).indirect(key_list[:]))
-        q_picked = sb.tile([P, PACK, B * NQ], F32, name="q_picked")
+        q_picked = sb.tile([P, PACK, B * NQ], F32, name="q_picked", tag="queries_then_bias")
         for t in range(3):
             nc.vector.tensor_copy(q_picked[:, t, :], q_front[:, t * TQ : (t + 1) * TQ].indirect(query_list[:]))
         for b in range(B):
@@ -87,14 +88,12 @@ def tile_attend_lq_score_kernel(tc, qT, k_words, k_scales, kb, offq, offs, out):
             for c in range(4):
                 nc.tensor.transpose(turned[:, c, :], bias_row[:, b * N + c * P : b * N + (c + 1) * P], ident[:])
             nc.scalar.copy(bias_col[:, 4 * b : 4 * b + 4], turned[:, :, P - 1])
-        bias = []
+        bias = sb.tile([P, B, N], F32, name="bias", tag="queries_then_bias")
         for b in range(B):
             spread = ps.tile([P, 4, P], F32, name="spread%d" % b)
             for c in range(4):
                 nc.tensor.transpose(spread[:, c, :], bias_col[:, 4 * b + c : 4 * b + c + 1].to_broadcast([P, P]), ident[:])
-            bias_b = sb.tile([P, N], F32, name="bias%d" % b)
-            nc.scalar.copy(bias_b[:], spread[:].rearrange("p c n -> p (c n)"))
-            bias.append(bias_b)
+            nc.scalar.copy(bias[:, b, :], spread[:].rearrange("p c n -> p (c n)"))
 
         H = N // 2
         pieces = []
@@ -118,8 +117,10 @@ def tile_attend_lq_score_kernel(tc, qT, k_words, k_scales, kb, offq, offs, out):
                     stop=True,
                 )
                 pieces.append((b, slice(lo + c, lo + c + width), acc))
-        for i, (b, cols, acc) in enumerate(pieces):
-            result = sb.tile([P, cols.stop - cols.start], F32, name="result%d" % i)
-            nc.vector.tensor_tensor(result[:], acc[:], bias[b][:, cols], ADD)
-            queue = nc.sync if i % 2 == 0 else nc.scalar
-            queue.dma_start(out[b, :, cols], result[:])
+        results = [sb.tile([P, H], F32, name="result%d" % g) for g in range(2 * B)]
+        for b, cols, acc in pieces:
+            g, lo = 2 * b + cols.start // H, cols.start % H
+            nc.vector.tensor_tensor(results[g][:, lo : lo + cols.stop - cols.start], acc[:], bias[:, b, cols], ADD)
+            if cols.stop % H == 0:
+                queue = nc.scalar if g % 2 == 0 else nc.sync
+                queue.dma_start(out[b, :, cols.stop - H : cols.stop], results[g][:])

@@ -57,21 +57,28 @@ def tile_attend_lq_score_kernel(tc, qT, k_words, k_scales, kb, offq, offs, out):
         nc.vector.tensor_copy(bias_row[:], bias_pool[:].indirect(key_list[:]))
         key_scales = sb.tile([P, B * N], U8, name="key_scales", align_bytes=64)
         nc.vector.tensor_copy(key_scales[:], scale_pool[:].bitcast(U8).indirect(key_list[:]))
-        q_picked = sb.tile([P, PACK, B * NQ], F32, name="q_picked", tag="queries_then_bias")
-        for t in range(3):
-            nc.vector.tensor_copy(q_picked[:, t, :], q_front[:, t * TQ : (t + 1) * TQ].indirect(query_list[:]))
+        q_picked = sb.tile([P, B, PACK, NQ], BF16, name="q_picked", tag="queries_then_bias")
+        q_rounded = sb.tile([P, TQ], BF16, name="q_rounded", tag="rounded_then_columns")
+        for lo in (0, HEAD):
+            nc.scalar.copy(q_rounded[:, lo : lo + HEAD], q_front[:, lo : lo + HEAD])
+        nc.scalar.activation(q_picked[:, :, 0, :], q_rounded[:].indirect(query_list[:]), mybir.ActivationFunctionType.Copy)
+        for t in (1, 2):
+            nc.vector.tensor_copy(q_picked[:, :, t, :], q_front[:, t * TQ : (t + 1) * TQ].indirect(query_list[:]))
         for b in range(B):
             nc.vector.tensor_copy(
-                q_picked[:, 3, b * NQ : (b + 1) * NQ],
+                q_picked[:, b, 3, :],
                 q_last[:].indirect(query_list[:, b * NQ // 16 : (b + 1) * NQ // 16]),
             )
 
         q_grouped = [sb.tile([P, NQ, PACK], BF16, name="q_grouped%d" % b, align_bytes=64) for b in range(B)]
-        for b in range(B):
-            weave = nc.scalar.copy if b == 0 else nc.vector.tensor_copy
+        for weave, b, lo, hi in (
+            (nc.scalar.copy, 0, 0, NQ // 2),
+            (nc.vector.tensor_copy, 0, NQ // 2, NQ),
+            (nc.vector.tensor_copy, 1, 0, NQ),
+        ):
             weave(
-                q_grouped[b][:].rearrange("p (c i) t -> p c t i", i=4),
-                q_picked[:, :, b * NQ : (b + 1) * NQ].rearrange("p t (c i) -> p c t i", i=4),
+                q_grouped[b][:, lo:hi, :].rearrange("p (c i) t -> p c t i", i=4),
+                q_picked[:, b, :, lo:hi].rearrange("p t (c i) -> p c t i", i=4),
             )
         q_codes = sb.tile([P, B * NQ], U32, name="q_codes", align_bytes=64)
         q_scales = sb.tile([P, B * NQ], U8, name="q_scales", align_bytes=64)
@@ -82,7 +89,7 @@ def tile_attend_lq_score_kernel(tc, qT, k_words, k_scales, kb, offq, offs, out):
                 in_=q_grouped[b][:].rearrange("p n t -> p (n t)"),
             )
 
-        bias_col = sb.tile([P, B * N // P], F32, name="bias_col")
+        bias_col = sb.tile([P, B * N // P], F32, name="bias_col", tag="rounded_then_columns")
         for b in range(B):
             turned = ps.tile([P, 4, P], F32, name="turned%d" % b, tag="turned%d" % b)
             for c in range(4):

@@ -40,23 +40,23 @@ def tile_attend_lq_score_kernel(tc, qT, k_words, k_scales, kb, offq, offs, out):
 
         q_rows = qT.rearrange("(p t) n -> p (t n)", t=PACK)
         HEAD = TQ // 2
-        scale_rows = k_scales[0].bitcast(I32).rearrange("(quad r) n -> r quad n", r=4)
         nc.sync.dma_start(key_list[:], offs)
         nc.sync.dma_start(q_front[:, 0:HEAD], q_rows[:, 0:HEAD])
-        for r in range(4):
-            queue = nc.sync if r < 2 else nc.scalar
-            queue.dma_start(scale_pool[r:P:32, :], scale_rows[r])
+        nc.sync.dma_start(scale_pool[0:P:8, :], k_scales[0].bitcast(I32))
         nc.sync.dma_start(bias_pool[P - 1 : P, :], kb[0:1, :])
-        nc.sync.dma_start(q_front[:, HEAD : HEAD + 2 * TQ], q_rows[:, HEAD : HEAD + 2 * TQ])
+        nc.sync.dma_start(q_front[:, HEAD:], q_rows[:, HEAD : 3 * TQ])
         nc.sync.dma_start(query_list[:], offq)
-        nc.sync.dma_start(q_front[:, HEAD + 2 * TQ :], q_rows[:, HEAD + 2 * TQ : 3 * TQ])
         nc.sync.dma_start(q_last[:], q_rows[:, 3 * TQ :])
         nc.sync.dma_start(word_pool[:], k_words[0].rearrange("p t r -> p (t r)").bitcast(I32))
 
         bias_row = sb.tile([P, B * N], F32, name="bias_row")
         nc.vector.tensor_copy(bias_row[:], bias_pool[:].indirect(key_list[:]))
+        picked_scales = sb.tile([P, B * N], U8, name="picked_scales")
+        nc.vector.tensor_copy(picked_scales[:], scale_pool[:].bitcast(U8).indirect(key_list[:]))
         key_scales = sb.tile([P, B * N], U8, name="key_scales", align_bytes=64)
-        nc.vector.tensor_copy(key_scales[:], scale_pool[:].bitcast(U8).indirect(key_list[:]))
+        nc.vector.memset(key_scales[:].bitcast(I32), 0)
+        for r in range(4):
+            nc.sync.dma_start(key_scales[:].bitcast(I32)[r:P:32, :], picked_scales[:].bitcast(I32)[8 * r : P : 32, :])
         q_picked = sb.tile([P, B, PACK, NQ], BF16, name="q_picked", tag="queries_then_bias")
         q_rounded = sb.tile([P, TQ], BF16, name="q_rounded", tag="rounded_then_columns")
         for lo in (0, HEAD):

@@ -35,17 +35,18 @@ def tile_attend_lq_score_kernel(tc, qT, k_words, k_scales, kb, offq, offs, out):
         ident = sb.tile([P, P], F32, name="ident")
 
         nc.vector.memset(scale_pool[:], 0)
+        nc.vector.memset(ident[:], 0.0)
         nc.vector.memset(bias_pool[0 : P - 1, :], 0.0)
-        make_identity(nc, ident[:])
+        make_identity(nc, ident[:], nomemset=True)
 
         q_rows = qT.rearrange("(p t) n -> p (t n)", t=PACK)
         HEAD = TQ // 2
         nc.sync.dma_start(key_list[:], offs)
         nc.sync.dma_start(q_front[:, 0:HEAD], q_rows[:, 0:HEAD])
-        nc.sync.dma_start(scale_pool[0:P:8, :], k_scales[0].bitcast(I32))
         nc.sync.dma_start(bias_pool[P - 1 : P, :], kb[0:1, :])
-        nc.sync.dma_start(q_front[:, HEAD:], q_rows[:, HEAD : 3 * TQ])
         nc.sync.dma_start(query_list[:], offq)
+        nc.sync.dma_start(scale_pool[0:P:8, :], k_scales[0].bitcast(I32))
+        nc.sync.dma_start(q_front[:, HEAD:], q_rows[:, HEAD : 3 * TQ])
         nc.sync.dma_start(q_last[:], q_rows[:, 3 * TQ :])
         nc.sync.dma_start(word_pool[:], k_words[0].rearrange("p t r -> p (t r)").bitcast(I32))
 

@@ -45,7 +45,7 @@ def tile_attend_lq_score_kernel(tc, qT, k_words, k_scales, kb, offq, offs, out):
         nc.sync.dma_start(q_front[:, 0:HEAD], q_rows[:, 0:HEAD])
         nc.sync.dma_start(bias_pool[P - 1 : P, :], kb[0:1, :])
         nc.sync.dma_start(query_list[:], offq)
-        nc.sync.dma_start(scale_pool[0:P:8, :], k_scales[0].bitcast(I32))
+        nc.sync.dma_start(scale_pool[32:96:4, :], k_scales[0].bitcast(I32))
         nc.sync.dma_start(q_front[:, HEAD:], q_rows[:, HEAD : 3 * TQ])
         nc.sync.dma_start(q_last[:], q_rows[:, 3 * TQ :])
         nc.sync.dma_start(word_pool[:], k_words[0].rearrange("p t r -> p (t r)").bitcast(I32))
@@ -57,7 +57,7 @@ def tile_attend_lq_score_kernel(tc, qT, k_words, k_scales, kb, offq, offs, out):
         key_scales = sb.tile([P, B * N], U8, name="key_scales", align_bytes=64)
         nc.vector.memset(key_scales[:].bitcast(I32), 0)
         for r in range(4):
-            nc.sync.dma_start(key_scales[:].bitcast(I32)[r:P:32, :], picked_scales[:].bitcast(I32)[8 * r : P : 32, :])
+            nc.sync.dma_start(key_scales[:].bitcast(I32)[r:P:32, :], picked_scales[:].bitcast(I32)[32 + 4 * r : 96 : 16, :])
         q_picked = sb.tile([P, B, PACK, NQ], BF16, name="q_picked", tag="queries_then_bias")
         q_rounded = sb.tile([P, TQ], BF16, name="q_rounded", tag="rounded_then_columns")
         for lo in (0, HEAD):
@@ -105,16 +105,17 @@ def tile_attend_lq_score_kernel(tc, qT, k_words, k_scales, kb, offq, offs, out):
 
         H = N // 2
         pieces = []
+        banks = ["scores0", "scores1", "scores2", "scores3", "turned0", "turned1", "spread0", "spread1"]
         for g in range(2 * B):
             b, lo = g // 2, g % 2 * H
             key_words = sb.tile([P, H], U32, name="key_words%d" % g, align_bytes=64)
             nc.vector.tensor_copy(
                 key_words[:], word_pool[:].bitcast(U32).indirect(key_list[:, g * H // 16 : (g + 1) * H // 16])
             )
-            width = H // 2 if g == 2 * B - 1 else H
+            width = H // 2
             for c in range(0, H, width):
                 i = len(pieces)
-                acc = ps.tile([P, width], F32, name="scores%d" % i, tag="turned0" if i == 4 else "scores%d" % i)
+                acc = ps.tile([P, width], F32, name="scores%d" % i, tag=banks[i])
                 nc.tensor.matmul_mx(
                     out=acc[:],
                     lhsT=q_codes[:, b * NQ : (b + 1) * NQ].bitcast(FP8X4),

@@ -41,12 +41,12 @@ def tile_attend_lq_score_kernel(tc, qT, k_words, k_scales, kb, offq, offs, out):
 
         q_rows = qT.rearrange("(p t) n -> p (t n)", t=PACK)
         HEAD = TQ // 2
-        nc.sync.dma_start(key_list[:], offs)
         nc.sync.dma_start(q_front[:, 0:HEAD], q_rows[:, 0:HEAD])
+        nc.sync.dma_start(key_list[:], offs)
         nc.sync.dma_start(bias_pool[P - 1 : P, :], kb[0:1, :])
-        nc.sync.dma_start(query_list[:], offq)
         nc.sync.dma_start(scale_pool[32:96:4, :], k_scales[0].bitcast(I32))
         nc.sync.dma_start(q_front[:, HEAD:], q_rows[:, HEAD : 3 * TQ])
+        nc.sync.dma_start(query_list[:], offq)
         nc.sync.dma_start(q_last[:], q_rows[:, 3 * TQ :])
         nc.sync.dma_start(word_pool[:], k_words[0].rearrange("p t r -> p (t r)").bitcast(I32))
 

@@ -17,6 +17,7 @@ U16 = mybir.dt.uint16
 U8 = mybir.dt.uint8
 FP8X4 = mybir.dt.float8_e4m3fn_x4
 ADD = mybir.AluOpType.add
+COPY = mybir.ActivationFunctionType.Copy
 
 
 def tile_attend_lq_score_kernel(tc, qT, k_words, k_scales, kb, offq, offs, out):
@@ -27,44 +28,54 @@ def tile_attend_lq_score_kernel(tc, qT, k_words, k_scales, kb, offq, offs, out):
 
         key_list = sb.tile([P, B * N // 16], U16, name="key_list")
         query_list = sb.tile([P, B * NQ // 16], U16, name="query_list")
-        q_front = sb.tile([P, 3 * TQ], F32, name="q_front")
+        q_first = sb.tile([P, TQ], F32, name="q_first")
+        q_middle = sb.tile([P, 2 * TQ], F32, name="q_middle")
         q_last = sb.tile([P, TQ], F32, name="q_last")
         word_pool = sb.tile([P, T], I32, name="word_pool")
         scale_pool = sb.tile([P, T // 4], I32, name="scale_pool", align_bytes=64)
-        bias_pool = sb.tile([P, T], F32, name="bias_pool")
+        bias_rows = sb.tile([P, P], F32, name="bias_rows")
         ident = sb.tile([P, P], F32, name="ident")
 
+        nc.vector.memset(bias_rows[:], 0.0)
         nc.vector.memset(scale_pool[:], 0)
         nc.vector.memset(ident[:], 0.0)
-        nc.vector.memset(bias_pool[0 : P - 1, :], 0.0)
         make_identity(nc, ident[:], nomemset=True)
 
         q_rows = qT.rearrange("(p t) n -> p (t n)", t=PACK)
-        HEAD = TQ // 2
-        nc.sync.dma_start(q_front[:, 0:HEAD], q_rows[:, 0:HEAD])
+        nc.sync.dma_start(q_first[:], q_rows[:, 0:TQ])
         nc.sync.dma_start(key_list[:], offs)
-        nc.sync.dma_start(bias_pool[P - 1 : P, :], kb[0:1, :])
-        nc.sync.dma_start(scale_pool[32:96:4, :], k_scales[0].bitcast(I32))
-        nc.sync.dma_start(q_front[:, HEAD:], q_rows[:, HEAD : 3 * TQ])
         nc.sync.dma_start(query_list[:], offq)
+        nc.sync.dma_start(bias_rows[32:96:4, :], kb[0].rearrange("(j n) -> j n", n=P))
+        nc.sync.dma_start(scale_pool[32:96:4, :], k_scales[0].bitcast(I32))
+        nc.sync.dma_start(q_middle[:], q_rows[:, TQ : 3 * TQ])
         nc.sync.dma_start(q_last[:], q_rows[:, 3 * TQ :])
         nc.sync.dma_start(word_pool[:], k_words[0].rearrange("p t r -> p (t r)").bitcast(I32))
 
-        bias_row = sb.tile([P, B * N], F32, name="bias_row")
-        nc.vector.tensor_copy(bias_row[:], bias_pool[:].indirect(key_list[:]))
+        q_picked = sb.tile([P, B, PACK, NQ], BF16, name="q_picked")
+        nc.vector.tensor_copy(q_picked[:, :, 0, :], q_first[:].indirect(query_list[:]))
         picked_scales = sb.tile([P, B * N], U8, name="picked_scales")
         nc.vector.tensor_copy(picked_scales[:], scale_pool[:].bitcast(U8).indirect(key_list[:]))
         key_scales = sb.tile([P, B * N], U8, name="key_scales", align_bytes=64)
         nc.vector.memset(key_scales[:].bitcast(I32), 0)
         for r in range(4):
             nc.sync.dma_start(key_scales[:].bitcast(I32)[r:P:32, :], picked_scales[:].bitcast(I32)[32 + 4 * r : 96 : 16, :])
-        q_picked = sb.tile([P, B, PACK, NQ], BF16, name="q_picked", tag="queries_then_bias")
-        q_rounded = sb.tile([P, TQ], BF16, name="q_rounded", tag="rounded_then_columns")
-        for lo in (0, HEAD):
-            nc.scalar.copy(q_rounded[:, lo : lo + HEAD], q_front[:, lo : lo + HEAD])
-        nc.scalar.activation(q_picked[:, :, 0, :], q_rounded[:].indirect(query_list[:]), mybir.ActivationFunctionType.Copy)
+
+        turned = ps.tile([P, P], F32, name="turned", tag="bank7")
+        nc.tensor.transpose(turned[:], bias_rows[:], ident[:])
+        bias_cols = sb.tile([P, T // P], F32, name="bias_cols")
+        nc.scalar.copy(bias_cols[:], turned[:, 32:96:4])
+        bias_pool = sb.tile([P, T], F32, name="bias_pool")
+        for g in range(T // N):
+            spread = ps.tile([P, 4, P], F32, name="spread%d" % g, tag="bank%d" % g)
+            for j in range(4):
+                nc.tensor.transpose(spread[:, j, :], bias_cols[:, 4 * g + j : 4 * g + j + 1].to_broadcast([P, P]), ident[:])
+            nc.scalar.copy(bias_pool[:, g * N : (g + 1) * N], spread[:].rearrange("p j n -> p (j n)"))
+        bias = sb.tile([P, B, N], F32, name="bias")
+        for b in range(B):
+            nc.scalar.activation(bias[:, b, :], bias_pool[:].indirect(key_list[:, b * N // 16 : (b + 1) * N // 16]), COPY)
+
         for t in (1, 2):
-            nc.vector.tensor_copy(q_picked[:, :, t, :], q_front[:, t * TQ : (t + 1) * TQ].indirect(query_list[:]))
+            nc.vector.tensor_copy(q_picked[:, :, t, :], q_middle[:, (t - 1) * TQ : t * TQ].indirect(query_list[:]))
         for b in range(B):
             nc.vector.tensor_copy(
                 q_picked[:, b, 3, :],
@@ -72,14 +83,10 @@ def tile_attend_lq_score_kernel(tc, qT, k_words, k_scales, kb, offq, offs, out):
             )
 
         q_grouped = [sb.tile([P, NQ, PACK], BF16, name="q_grouped%d" % b, align_bytes=64) for b in range(B)]
-        for weave, b, lo, hi in (
-            (nc.scalar.copy, 0, 0, NQ // 2),
-            (nc.vector.tensor_copy, 0, NQ // 2, NQ),
-            (nc.vector.tensor_copy, 1, 0, NQ),
-        ):
-            weave(
-                q_grouped[b][:, lo:hi, :].rearrange("p (c i) t -> p c t i", i=4),
-                q_picked[:, b, :, lo:hi].rearrange("p t (c i) -> p c t i", i=4),
+        for b in range(B):
+            nc.vector.tensor_copy(
+                q_grouped[b][:].rearrange("p (c i) t -> p c t i", i=4),
+                q_picked[:, b, :, :].rearrange("p t (c i) -> p c t i", i=4),
             )
         q_codes = sb.tile([P, B * NQ], U32, name="q_codes", align_bytes=64)
         q_scales = sb.tile([P, B * NQ], U8, name="q_scales", align_bytes=64)
@@ -90,22 +97,8 @@ def tile_attend_lq_score_kernel(tc, qT, k_words, k_scales, kb, offq, offs, out):
                 in_=q_grouped[b][:].rearrange("p n t -> p (n t)"),
             )
 
-        bias_col = sb.tile([P, B * N // P], F32, name="bias_col", tag="rounded_then_columns")
-        for b in range(B):
-            turned = ps.tile([P, 4, P], F32, name="turned%d" % b, tag="turned%d" % b)
-            for c in range(4):
-                nc.tensor.transpose(turned[:, c, :], bias_row[:, b * N + c * P : b * N + (c + 1) * P], ident[:])
-            nc.scalar.copy(bias_col[:, 4 * b : 4 * b + 4], turned[:, :, P - 1])
-        bias = sb.tile([P, B, N], F32, name="bias", tag="queries_then_bias")
-        for b in range(B):
-            spread = ps.tile([P, 4, P], F32, name="spread%d" % b)
-            for c in range(4):
-                nc.tensor.transpose(spread[:, c, :], bias_col[:, 4 * b + c : 4 * b + c + 1].to_broadcast([P, P]), ident[:])
-            nc.scalar.copy(bias[:, b, :], spread[:].rearrange("p c n -> p (c n)"))
-
         H = N // 2
         pieces = []
-        banks = ["scores0", "scores1", "scores2", "scores3", "turned0", "turned1", "spread0", "spread1"]
         for g in range(2 * B):
             b, lo = g // 2, g % 2 * H
             key_words = sb.tile([P, H], U32, name="key_words%d" % g, align_bytes=64)
@@ -115,7 +108,7 @@ def tile_attend_lq_score_kernel(tc, qT, k_words, k_scales, kb, offq, offs, out):
             width = H // 2
             for c in range(0, H, width):
                 i = len(pieces)
-                acc = ps.tile([P, width], F32, name="scores%d" % i, tag=banks[i])
+                acc = ps.tile([P, width], F32, name="scores%d" % i, tag="bank%d" % i)
                 nc.tensor.matmul_mx(
                     out=acc[:],
                     lhsT=q_codes[:, b * NQ : (b + 1) * NQ].bitcast(FP8X4),

@@ -28,8 +28,7 @@ def tile_attend_lq_score_kernel(tc, qT, k_words, k_scales, kb, offq, offs, out):
 
         key_list = sb.tile([P, B * N // 16], U16, name="key_list")
         query_list = sb.tile([P, B * NQ // 16], U16, name="query_list")
-        q_first = sb.tile([P, TQ], F32, name="q_first")
-        q_middle = sb.tile([P, 2 * TQ], F32, name="q_middle")
+        q_front = sb.tile([P, 3 * TQ], F32, name="q_front")
         q_last = sb.tile([P, TQ], F32, name="q_last")
         word_pool = sb.tile([P, T], I32, name="word_pool")
         scale_pool = sb.tile([P, T // 4], I32, name="scale_pool", align_bytes=64)
@@ -42,17 +41,16 @@ def tile_attend_lq_score_kernel(tc, qT, k_words, k_scales, kb, offq, offs, out):
         make_identity(nc, ident[:], nomemset=True)
 
         q_rows = qT.rearrange("(p t) n -> p (t n)", t=PACK)
-        nc.sync.dma_start(q_first[:], q_rows[:, 0:TQ])
+        HEAD = TQ // 2
+        nc.sync.dma_start(q_front[:, 0:HEAD], q_rows[:, 0:HEAD])
         nc.sync.dma_start(key_list[:], offs)
-        nc.sync.dma_start(query_list[:], offq)
         nc.sync.dma_start(bias_rows[32:96:4, :], kb[0].rearrange("(j n) -> j n", n=P))
         nc.sync.dma_start(scale_pool[32:96:4, :], k_scales[0].bitcast(I32))
-        nc.sync.dma_start(q_middle[:], q_rows[:, TQ : 3 * TQ])
+        nc.sync.dma_start(q_front[:, HEAD:], q_rows[:, HEAD : 3 * TQ])
+        nc.sync.dma_start(query_list[:], offq)
         nc.sync.dma_start(q_last[:], q_rows[:, 3 * TQ :])
         nc.sync.dma_start(word_pool[:], k_words[0].rearrange("p t r -> p (t r)").bitcast(I32))
 
-        q_picked = sb.tile([P, B, PACK, NQ], BF16, name="q_picked")
-        nc.vector.tensor_copy(q_picked[:, :, 0, :], q_first[:].indirect(query_list[:]))
         picked_scales = sb.tile([P, B * N], U8, name="picked_scales")
         nc.vector.tensor_copy(picked_scales[:], scale_pool[:].bitcast(U8).indirect(key_list[:]))
         key_scales = sb.tile([P, B * N], U8, name="key_scales", align_bytes=64)
@@ -62,27 +60,44 @@ def tile_attend_lq_score_kernel(tc, qT, k_words, k_scales, kb, offq, offs, out):
 
         turned = ps.tile([P, P], F32, name="turned", tag="bank7")
         nc.tensor.transpose(turned[:], bias_rows[:], ident[:])
-        bias_cols = sb.tile([P, T // P], F32, name="bias_cols")
-        nc.scalar.copy(bias_cols[:], turned[:, 32:96:4])
+        bias_cols = [
+            sb.tile([P, 8], F32, name="bias_cols0", tag="columns_then_queries"),
+            sb.tile([P, 8], F32, name="bias_cols1"),
+        ]
+        for h in range(2):
+            nc.scalar.copy(bias_cols[h][:], turned[:, 32 + 32 * h : 64 + 32 * h : 4])
         bias_pool = sb.tile([P, T], F32, name="bias_pool")
-        for g in range(T // N):
+
+        def spread_bias(g):
             spread = ps.tile([P, 4, P], F32, name="spread%d" % g, tag="bank%d" % g)
             for j in range(4):
-                nc.tensor.transpose(spread[:, j, :], bias_cols[:, 4 * g + j : 4 * g + j + 1].to_broadcast([P, P]), ident[:])
+                col = 4 * (g % 2) + j
+                nc.tensor.transpose(spread[:, j, :], bias_cols[g // 2][:, col : col + 1].to_broadcast([P, P]), ident[:])
             nc.scalar.copy(bias_pool[:, g * N : (g + 1) * N], spread[:].rearrange("p j n -> p (j n)"))
+
+        spread_bias(0)
+        spread_bias(1)
+        q_picked = sb.tile([P, B, PACK, NQ], BF16, name="q_picked", tag="columns_then_queries")
+        for b in range(B):
+            nc.scalar.activation(q_picked[:, b, 0, :], q_front[:].indirect(query_list[:, b * NQ // 16 : (b + 1) * NQ // 16]), COPY)
+        spread_bias(2)
+        spread_bias(3)
         bias = sb.tile([P, B, N], F32, name="bias")
         for b in range(B):
             nc.scalar.activation(bias[:, b, :], bias_pool[:].indirect(key_list[:, b * N // 16 : (b + 1) * N // 16]), COPY)
 
         for t in (1, 2):
-            nc.vector.tensor_copy(q_picked[:, :, t, :], q_middle[:, (t - 1) * TQ : t * TQ].indirect(query_list[:]))
+            nc.vector.tensor_copy(q_picked[:, :, t, :], q_front[:, t * TQ : (t + 1) * TQ].indirect(query_list[:]))
         for b in range(B):
             nc.vector.tensor_copy(
                 q_picked[:, b, 3, :],
                 q_last[:].indirect(query_list[:, b * NQ // 16 : (b + 1) * NQ // 16]),
             )
 
-        q_grouped = [sb.tile([P, NQ, PACK], BF16, name="q_grouped%d" % b, align_bytes=64) for b in range(B)]
+        q_grouped = [
+            sb.tile([P, NQ, PACK], BF16, name="q_grouped0", align_bytes=64),
+            sb.tile([P, NQ, PACK], BF16, name="q_grouped1", tag="grouped_then_words", align_bytes=64),
+        ]
         for b in range(B):
             nc.vector.tensor_copy(
                 q_grouped[b][:].rearrange("p (c i) t -> p c t i", i=4),
@@ -99,11 +114,11 @@ def tile_attend_lq_score_kernel(tc, qT, k_words, k_scales, kb, offq, offs, out):
 
         H = N // 2
         pieces = []
+        key_words = sb.tile([P, B * N], U32, name="key_words", tag="grouped_then_words", align_bytes=64)
         for g in range(2 * B):
             b, lo = g // 2, g % 2 * H
-            key_words = sb.tile([P, H], U32, name="key_words%d" % g, align_bytes=64)
             nc.vector.tensor_copy(
-                key_words[:], word_pool[:].bitcast(U32).indirect(key_list[:, g * H // 16 : (g + 1) * H // 16])
+                key_words[:, g * H : (g + 1) * H], word_pool[:].bitcast(U32).indirect(key_list[:, g * H // 16 : (g + 1) * H // 16])
             )
             width = H // 2
             for c in range(0, H, width):
@@ -113,7 +128,7 @@ def tile_attend_lq_score_kernel(tc, qT, k_words, k_scales, kb, offq, offs, out):
                     out=acc[:],
                     lhsT=q_codes[:, b * NQ : (b + 1) * NQ].bitcast(FP8X4),
                     lhsT_scale=q_scales[:, b * NQ : (b + 1) * NQ],
-                    rhs=key_words[:, c : c + width].bitcast(FP8X4),
+                    rhs=key_words[:, g * H + c : g * H + c + width].bitcast(FP8X4),
                     rhs_scale=key_scales[:, b * N + lo + c : b * N + lo + c + width],
                     start=True,
                     stop=True,

@@ -60,31 +60,27 @@ def tile_attend_lq_score_kernel(tc, qT, k_words, k_scales, kb, offq, offs, out):
 
         turned = ps.tile([P, P], F32, name="turned", tag="bank7")
         nc.tensor.transpose(turned[:], bias_rows[:], ident[:])
-        bias_cols = [
-            sb.tile([P, 8], F32, name="bias_cols0", tag="columns_then_queries"),
-            sb.tile([P, 8], F32, name="bias_cols1"),
-        ]
-        for h in range(2):
-            nc.scalar.copy(bias_cols[h][:], turned[:, 32 + 32 * h : 64 + 32 * h : 4])
-        bias_pool = sb.tile([P, T], F32, name="bias_pool")
-
-        def spread_bias(g):
-            spread = ps.tile([P, 4, P], F32, name="spread%d" % g, tag="bank%d" % g)
-            for j in range(4):
-                col = 4 * (g % 2) + j
-                nc.tensor.transpose(spread[:, j, :], bias_cols[g // 2][:, col : col + 1].to_broadcast([P, P]), ident[:])
-            nc.scalar.copy(bias_pool[:, g * N : (g + 1) * N], spread[:].rearrange("p j n -> p (j n)"))
-
-        spread_bias(0)
-        spread_bias(1)
+        first_cols = sb.tile([P, 4], F32, name="first_cols", tag="columns_then_queries")
+        other_cols = sb.tile([P, 12], F32, name="other_cols")
+        nc.scalar.copy(first_cols[:], turned[:, 32:48:4])
+        nc.scalar.copy(other_cols[:], turned[:, 48:96:4])
+        columns = [first_cols[:, j : j + 1] for j in range(4)] + [other_cols[:, j : j + 1] for j in range(12)]
+        banks = [ps.tile([P, 4, P], F32, name="spread%d" % g, tag="bank%d" % g) for g in range(T // N)]
+        for j, column in enumerate(columns):
+            nc.tensor.transpose(banks[j // 4][:, j % 4, :], column.to_broadcast([P, P]), ident[:])
         q_picked = sb.tile([P, B, PACK, NQ], BF16, name="q_picked", tag="columns_then_queries")
         for b in range(B):
             nc.scalar.activation(q_picked[:, b, 0, :], q_front[:].indirect(query_list[:, b * NQ // 16 : (b + 1) * NQ // 16]), COPY)
-        spread_bias(2)
-        spread_bias(3)
+        bias_pool = sb.tile([P, T], F32, name="bias_pool")
+        for g in range(T // N):
+            nc.scalar.copy(bias_pool[:, g * N : (g + 1) * N], banks[g][:].rearrange("p j n -> p (j n)"))
         bias = sb.tile([P, B, N], F32, name="bias")
-        for b in range(B):
-            nc.scalar.activation(bias[:, b, :], bias_pool[:].indirect(key_list[:, b * N // 16 : (b + 1) * N // 16]), COPY)
+        for g in range(2 * B):
+            nc.scalar.activation(
+                bias[:, g // 2, g % 2 * N // 2 : (g % 2 + 1) * N // 2],
+                bias_pool[:].indirect(key_list[:, g * N // 32 : (g + 1) * N // 32]),
+                COPY,
+            )
 
         for t in (1, 2):
             nc.vector.tensor_copy(q_picked[:, :, t, :], q_front[:, t * TQ : (t + 1) * TQ].indirect(query_list[:]))
@@ -95,8 +91,8 @@ def tile_attend_lq_score_kernel(tc, qT, k_words, k_scales, kb, offq, offs, out):
             )
 
         q_grouped = [
-            sb.tile([P, NQ, PACK], BF16, name="q_grouped0", align_bytes=64),
-            sb.tile([P, NQ, PACK], BF16, name="q_grouped1", tag="grouped_then_words", align_bytes=64),
+            sb.tile([P, NQ, PACK], BF16, name="q_grouped0", tag="grouped_then_words", align_bytes=64),
+            sb.tile([P, NQ, PACK], BF16, name="q_grouped1", align_bytes=64),
         ]
         for b in range(B):
             nc.vector.tensor_copy(
@@ -113,31 +109,30 @@ def tile_attend_lq_score_kernel(tc, qT, k_words, k_scales, kb, offq, offs, out):
             )
 
         H = N // 2
-        pieces = []
+        WIDTH = 128
         key_words = sb.tile([P, B * N], U32, name="key_words", tag="grouped_then_words", align_bytes=64)
-        for g in range(2 * B):
-            b, lo = g // 2, g % 2 * H
-            nc.vector.tensor_copy(
-                key_words[:, g * H : (g + 1) * H], word_pool[:].bitcast(U32).indirect(key_list[:, g * H // 16 : (g + 1) * H // 16])
-            )
-            width = H // 2
-            for c in range(0, H, width):
-                i = len(pieces)
-                acc = ps.tile([P, width], F32, name="scores%d" % i, tag="bank%d" % i)
+        cuts = [0, WIDTH] + list(range(H, B * N + 1, H))
+        scores = []
+        for lo, hi in zip(cuts, cuts[1:]):
+            nc.vector.tensor_copy(key_words[:, lo:hi], word_pool[:].bitcast(U32).indirect(key_list[:, lo // 16 : hi // 16]))
+            for c in range(lo, hi, WIDTH):
+                b = c // N
+                acc = ps.tile([P, WIDTH], F32, name="scores%d" % len(scores), tag="bank%d" % len(scores))
                 nc.tensor.matmul_mx(
                     out=acc[:],
                     lhsT=q_codes[:, b * NQ : (b + 1) * NQ].bitcast(FP8X4),
                     lhsT_scale=q_scales[:, b * NQ : (b + 1) * NQ],
-                    rhs=key_words[:, g * H + c : g * H + c + width].bitcast(FP8X4),
-                    rhs_scale=key_scales[:, b * N + lo + c : b * N + lo + c + width],
+                    rhs=key_words[:, c : c + WIDTH].bitcast(FP8X4),
+                    rhs_scale=key_scales[:, c : c + WIDTH],
                     start=True,
                     stop=True,
                 )
-                pieces.append((b, slice(lo + c, lo + c + width), acc))
+                scores.append(acc)
         results = [sb.tile([P, H], F32, name="result%d" % g) for g in range(2 * B)]
-        for b, cols, acc in pieces:
-            g, lo = 2 * b + cols.start // H, cols.start % H
-            nc.vector.tensor_tensor(results[g][:, lo : lo + cols.stop - cols.start], acc[:], bias[:, b, cols], ADD)
-            if cols.stop % H == 0:
-                queue = nc.scalar if g % 2 == 0 else nc.sync
-                queue.dma_start(out[b, :, cols.stop - H : cols.stop], results[g][:])
+        for i, acc in enumerate(scores):
+            g, lo = divmod(i * WIDTH, H)
+            b, col = divmod(i * WIDTH, N)
+            nc.vector.tensor_tensor(results[g][:, lo : lo + WIDTH], acc[:], bias[:, b, col : col + WIDTH], ADD)
+            if lo + WIDTH == H:
+                queue = nc.scalar if g == 2 else nc.sync
+                queue.dma_start(out[b, :, col + WIDTH - H : col + WIDTH], results[g][:])

@@ -60,19 +60,21 @@ def tile_attend_lq_score_kernel(tc, qT, k_words, k_scales, kb, offq, offs, out):
 
         turned = ps.tile([P, P], F32, name="turned", tag="bank7")
         nc.tensor.transpose(turned[:], bias_rows[:], ident[:])
-        first_cols = sb.tile([P, 4], F32, name="first_cols", tag="columns_then_queries")
-        other_cols = sb.tile([P, 12], F32, name="other_cols")
-        nc.scalar.copy(first_cols[:], turned[:, 32:48:4])
-        nc.scalar.copy(other_cols[:], turned[:, 48:96:4])
-        columns = [first_cols[:, j : j + 1] for j in range(4)] + [other_cols[:, j : j + 1] for j in range(12)]
+        first_cols = sb.tile([P, 8], F32, name="first_cols", tag="columns_then_queries")
+        other_cols = sb.tile([P, 8], F32, name="other_cols")
+        nc.scalar.copy(first_cols[:], turned[:, 32:64:4])
+        nc.scalar.copy(other_cols[:], turned[:, 64:96:4])
+        columns = [cols[:, j : j + 1] for cols in (first_cols, other_cols) for j in range(8)]
         banks = [ps.tile([P, 4, P], F32, name="spread%d" % g, tag="bank%d" % g) for g in range(T // N)]
         for j, column in enumerate(columns):
             nc.tensor.transpose(banks[j // 4][:, j % 4, :], column.to_broadcast([P, P]), ident[:])
+        bias_pool = sb.tile([P, T], F32, name="bias_pool")
+        for g in (0, 1):
+            nc.scalar.copy(bias_pool[:, g * N : (g + 1) * N], banks[g][:].rearrange("p j n -> p (j n)"))
         q_picked = sb.tile([P, B, PACK, NQ], BF16, name="q_picked", tag="columns_then_queries")
         for b in range(B):
             nc.scalar.activation(q_picked[:, b, 0, :], q_front[:].indirect(query_list[:, b * NQ // 16 : (b + 1) * NQ // 16]), COPY)
-        bias_pool = sb.tile([P, T], F32, name="bias_pool")
-        for g in range(T // N):
+        for g in (2, 3):
             nc.scalar.copy(bias_pool[:, g * N : (g + 1) * N], banks[g][:].rearrange("p j n -> p (j n)"))
         bias = sb.tile([P, B, N], F32, name="bias")
         for g in range(2 * B):

@@ -113,7 +113,7 @@ def tile_attend_lq_score_kernel(tc, qT, k_words, k_scales, kb, offq, offs, out):
         H = N // 2
         WIDTH = 128
         key_words = sb.tile([P, B * N], U32, name="key_words", tag="grouped_then_words", align_bytes=64)
-        cuts = [0, WIDTH] + list(range(H, B * N + 1, H))
+        cuts = list(range(0, B * N + 1, H))
         scores = []
         for lo, hi in zip(cuts, cuts[1:]):
             nc.vector.tensor_copy(key_words[:, lo:hi], word_pool[:].bitcast(U32).indirect(key_list[:, lo // 16 : hi // 16]))
@@ -136,5 +136,5 @@ def tile_attend_lq_score_kernel(tc, qT, k_words, k_scales, kb, offq, offs, out):
             b, col = divmod(i * WIDTH, N)
             nc.vector.tensor_tensor(results[g][:, lo : lo + WIDTH], acc[:], bias[:, b, col : col + WIDTH], ADD)
             if lo + WIDTH == H:
-                queue = nc.scalar if g == 2 else nc.sync
+                queue = nc.sync if g % 2 == 0 else nc.scalar
                 queue.dma_start(out[b, :, col + WIDTH - H : col + WIDTH], results[g][:])

@@ -18,6 +18,7 @@ U8 = mybir.dt.uint8
 FP8X4 = mybir.dt.float8_e4m3fn_x4
 ADD = mybir.AluOpType.add
 COPY = mybir.ActivationFunctionType.Copy
+ALIGN = 256
 
 
 def tile_attend_lq_score_kernel(tc, qT, k_words, k_scales, kb, offq, offs, out):
@@ -26,70 +27,63 @@ def tile_attend_lq_score_kernel(tc, qT, k_words, k_scales, kb, offq, offs, out):
         sb = ctx.enter_context(tc.tile_pool(name="sb", bufs=1))
         ps = ctx.enter_context(tc.psum_pool(name="ps", bufs=1))
 
-        key_list = sb.tile([P, B * N // 16], U16, name="key_list")
-        query_list = sb.tile([P, B * NQ // 16], U16, name="query_list")
-        q_front = sb.tile([P, 3 * TQ], F32, name="q_front")
-        q_last = sb.tile([P, TQ], F32, name="q_last")
-        word_pool = sb.tile([P, T], I32, name="word_pool")
-        scale_pool = sb.tile([P, T // 4], I32, name="scale_pool", align_bytes=64)
-        bias_rows = sb.tile([P, P], F32, name="bias_rows")
+        key_list = sb.tile([P, B * N // 16], U16, name="key_list", align_bytes=ALIGN)
+        query_list = sb.tile([P, B * NQ // 16], U16, name="query_list", align_bytes=ALIGN)
+        q_early = sb.tile([P, 2 * TQ], F32, name="q_early", align_bytes=ALIGN)
+        q_late = sb.tile([P, 2 * TQ], F32, name="q_late", align_bytes=ALIGN)
+        word_pool = sb.tile([P, T], I32, name="word_pool", align_bytes=ALIGN)
+        scale_pool = sb.tile([P, T // 4], I32, name="scale_pool", align_bytes=ALIGN)
+        RUN = T // P
+        bias_runs = sb.tile([P, RUN], F32, name="bias_runs", align_bytes=ALIGN)
         ident = sb.tile([P, P], F32, name="ident")
+        key_scales = sb.tile([P, B * N], U8, name="key_scales", align_bytes=ALIGN)
 
-        nc.vector.memset(bias_rows[:], 0.0)
         nc.vector.memset(scale_pool[:], 0)
         nc.vector.memset(ident[:], 0.0)
+        nc.vector.memset(key_scales[:].bitcast(I32), 0)
         make_identity(nc, ident[:], nomemset=True)
 
         q_rows = qT.rearrange("(p t) n -> p (t n)", t=PACK)
-        HEAD = TQ // 2
-        nc.sync.dma_start(q_front[:, 0:HEAD], q_rows[:, 0:HEAD])
-        nc.sync.dma_start(key_list[:], offs)
-        nc.sync.dma_start(bias_rows[32:96:4, :], kb[0].rearrange("(j n) -> j n", n=P))
-        nc.sync.dma_start(scale_pool[32:96:4, :], k_scales[0].bitcast(I32))
-        nc.sync.dma_start(q_front[:, HEAD:], q_rows[:, HEAD : 3 * TQ])
+        nc.sync.dma_start(q_early[:], q_rows[:, : 2 * TQ])
         nc.sync.dma_start(query_list[:], offq)
-        nc.sync.dma_start(q_last[:], q_rows[:, 3 * TQ :])
+        nc.sync.dma_start(bias_runs[:], kb[0].rearrange("(p j) -> p j", j=RUN))
+        nc.sync.dma_start(key_list[:], offs)
+        nc.sync.dma_start(scale_pool[32:96:4, :], k_scales[0].bitcast(I32))
+        nc.sync.dma_start(q_late[:], q_rows[:, 2 * TQ :])
         nc.sync.dma_start(word_pool[:], k_words[0].rearrange("p t r -> p (t r)").bitcast(I32))
 
-        picked_scales = sb.tile([P, B * N], U8, name="picked_scales")
+        q_picked = sb.tile([P, PACK, B * NQ], F32, name="q_picked")
+        for t in (0, 1):
+            nc.vector.tensor_copy(q_picked[:, t, :], q_early[:, t * TQ : (t + 1) * TQ].indirect(query_list[:]))
+
+        picked_scales = sb.tile([P, B * N], U8, name="picked_scales", align_bytes=ALIGN)
         nc.vector.tensor_copy(picked_scales[:], scale_pool[:].bitcast(U8).indirect(key_list[:]))
-        key_scales = sb.tile([P, B * N], U8, name="key_scales", align_bytes=64)
-        nc.vector.memset(key_scales[:].bitcast(I32), 0)
         for r in range(4):
             nc.sync.dma_start(key_scales[:].bitcast(I32)[r:P:32, :], picked_scales[:].bitcast(I32)[32 + 4 * r : 96 : 16, :])
 
-        turned = ps.tile([P, P], F32, name="turned", tag="bank7")
-        nc.tensor.transpose(turned[:], bias_rows[:], ident[:])
-        first_cols = sb.tile([P, 8], F32, name="first_cols", tag="columns_then_queries")
-        other_cols = sb.tile([P, 8], F32, name="other_cols")
-        nc.scalar.copy(first_cols[:], turned[:, 32:64:4])
-        nc.scalar.copy(other_cols[:], turned[:, 64:96:4])
-        columns = [cols[:, j : j + 1] for cols in (first_cols, other_cols) for j in range(8)]
-        banks = [ps.tile([P, 4, P], F32, name="spread%d" % g, tag="bank%d" % g) for g in range(T // N)]
-        for j, column in enumerate(columns):
-            nc.tensor.transpose(banks[j // 4][:, j % 4, :], column.to_broadcast([P, P]), ident[:])
+        banks = [ps.tile([P, 4, P], F32, name="spread%d" % g, tag="bank%d" % g) for g in range(RUN // 4)]
+        for j in range(RUN):
+            nc.tensor.transpose(banks[j // 4][:, j % 4, :], bias_runs[:, j : j + 1].to_broadcast([P, P]), ident[:])
         bias_pool = sb.tile([P, T], F32, name="bias_pool")
+        by_run = bias_pool[:].rearrange("m (p j) -> m p j", j=RUN)
+
+        def lay_out(g):
+            nc.scalar.copy(by_run[:, :, 4 * g : 4 * g + 4], banks[g][:].rearrange("m j p -> m p j"))
+
         for g in (0, 1):
-            nc.scalar.copy(bias_pool[:, g * N : (g + 1) * N], banks[g][:].rearrange("p j n -> p (j n)"))
-        q_picked = sb.tile([P, B, PACK, NQ], BF16, name="q_picked", tag="columns_then_queries")
+            lay_out(g)
         for b in range(B):
-            nc.scalar.activation(q_picked[:, b, 0, :], q_front[:].indirect(query_list[:, b * NQ // 16 : (b + 1) * NQ // 16]), COPY)
+            listed = query_list[:, b * NQ // 16 : (b + 1) * NQ // 16]
+            nc.vector.tensor_copy(q_picked[:, 2, b * NQ : (b + 1) * NQ], q_late[:, :TQ].indirect(listed))
+            nc.scalar.activation(q_picked[:, 3, b * NQ : (b + 1) * NQ], q_late[:, TQ:].indirect(listed), COPY)
         for g in (2, 3):
-            nc.scalar.copy(bias_pool[:, g * N : (g + 1) * N], banks[g][:].rearrange("p j n -> p (j n)"))
+            lay_out(g)
         bias = sb.tile([P, B, N], F32, name="bias")
         for g in range(2 * B):
             nc.scalar.activation(
                 bias[:, g // 2, g % 2 * N // 2 : (g % 2 + 1) * N // 2],
                 bias_pool[:].indirect(key_list[:, g * N // 32 : (g + 1) * N // 32]),
                 COPY,
-            )
-
-        for t in (1, 2):
-            nc.vector.tensor_copy(q_picked[:, :, t, :], q_front[:, t * TQ : (t + 1) * TQ].indirect(query_list[:]))
-        for b in range(B):
-            nc.vector.tensor_copy(
-                q_picked[:, b, 3, :],
-                q_last[:].indirect(query_list[:, b * NQ // 16 : (b + 1) * NQ // 16]),
             )
 
         q_grouped = [
@@ -99,7 +93,7 @@ def tile_attend_lq_score_kernel(tc, qT, k_words, k_scales, kb, offq, offs, out):
         for b in range(B):
             nc.vector.tensor_copy(
                 q_grouped[b][:].rearrange("p (c i) t -> p c t i", i=4),
-                q_picked[:, b, :, :].rearrange("p t (c i) -> p c t i", i=4),
+                q_picked[:, :, b * NQ : (b + 1) * NQ].rearrange("p t (c i) -> p c t i", i=4),
             )
         q_codes = sb.tile([P, B * NQ], U32, name="q_codes", align_bytes=64)
         q_scales = sb.tile([P, B * NQ], U8, name="q_scales", align_bytes=64)
@@ -130,7 +124,7 @@ def tile_attend_lq_score_kernel(tc, qT, k_words, k_scales, kb, offq, offs, out):
                     stop=True,
                 )
                 scores.append(acc)
-        results = [sb.tile([P, H], F32, name="result%d" % g) for g in range(2 * B)]
+        results = [sb.tile([P, H], F32, name="result%d" % g, align_bytes=ALIGN) for g in range(2 * B)]
         for i, acc in enumerate(scores):
             g, lo = divmod(i * WIDTH, H)
             b, col = divmod(i * WIDTH, N)

@@ -30,29 +30,44 @@ def tile_attend_lq_score_kernel(tc, qT, k_words, k_scales, kb, offq, offs, out):
         key_list = sb.tile([P, B * N // 16], U16, name="key_list", align_bytes=ALIGN)
         query_list = sb.tile([P, B * NQ // 16], U16, name="query_list", align_bytes=ALIGN)
         q_early = sb.tile([P, 2 * TQ], F32, name="q_early", align_bytes=ALIGN)
-        q_late = sb.tile([P, 2 * TQ], F32, name="q_late", align_bytes=ALIGN)
+        q_late = sb.tile([P, 2 * TQ], F32, name="q_late", tag="queries_then_bias", align_bytes=ALIGN)
         word_pool = sb.tile([P, T], I32, name="word_pool", align_bytes=ALIGN)
         scale_pool = sb.tile([P, T // 4], I32, name="scale_pool", align_bytes=ALIGN)
-        RUN = T // P
-        bias_runs = sb.tile([P, RUN], F32, name="bias_runs", align_bytes=ALIGN)
+        RUNS = T // P
+        bias_rows = sb.tile([P, P], F32, name="bias_rows", align_bytes=ALIGN)
         ident = sb.tile([P, P], F32, name="ident")
         key_scales = sb.tile([P, B * N], U8, name="key_scales", align_bytes=ALIGN)
 
-        nc.vector.memset(scale_pool[:], 0)
         nc.vector.memset(ident[:], 0.0)
+        nc.vector.memset(bias_rows[0:48, :], 0.0)
+        nc.vector.memset(bias_rows[64:P, :], 0.0)
+        nc.vector.memset(scale_pool[:], 0)
         nc.vector.memset(key_scales[:].bitcast(I32), 0)
         make_identity(nc, ident[:], nomemset=True)
 
         q_rows = qT.rearrange("(p t) n -> p (t n)", t=PACK)
+        nc.scalar.dma_start(bias_rows[48:64, :], kb[0].rearrange("(j n) -> j n", n=P))
         nc.sync.dma_start(q_early[:], q_rows[:, : 2 * TQ])
-        nc.sync.dma_start(query_list[:], offq)
-        nc.sync.dma_start(bias_runs[:], kb[0].rearrange("(p j) -> p j", j=RUN))
         nc.sync.dma_start(key_list[:], offs)
         nc.sync.dma_start(scale_pool[32:96:4, :], k_scales[0].bitcast(I32))
+        nc.sync.dma_start(query_list[:], offq)
         nc.sync.dma_start(q_late[:], q_rows[:, 2 * TQ :])
         nc.sync.dma_start(word_pool[:], k_words[0].rearrange("p t r -> p (t r)").bitcast(I32))
 
-        q_picked = sb.tile([P, PACK, B * NQ], F32, name="q_picked")
+        turned = ps.tile([P, P], F32, name="turned", tag="bank7")
+        nc.tensor.transpose(turned[:], bias_rows[:], ident[:])
+        first_cols = sb.tile([P, 12], F32, name="first_cols", tag="columns_then_queries")
+        other_cols = sb.tile([P, 4], F32, name="other_cols")
+        nc.scalar.copy(first_cols[:], turned[:, 48:60])
+        nc.scalar.copy(other_cols[:], turned[:, 60:64])
+        columns = [cols[:, j : j + 1] for cols in (first_cols, other_cols) for j in range(cols.shape[1])]
+        banks = [ps.tile([P, 4, P], F32, name="spread%d" % g, tag="bank%d" % g) for g in range(RUNS // 4)]
+        for j, column in enumerate(columns):
+            nc.tensor.transpose(banks[j // 4][:, j % 4, :], column.to_broadcast([P, P]), ident[:])
+        bias_pool = sb.tile([P, T], F32, name="bias_pool")
+        for g in (0, 1):
+            nc.scalar.copy(bias_pool[:, g * N : (g + 1) * N], banks[g][:].rearrange("p j n -> p (j n)"))
+        q_picked = sb.tile([P, PACK, B * NQ], F32, name="q_picked", tag="columns_then_queries")
         for t in (0, 1):
             nc.vector.tensor_copy(q_picked[:, t, :], q_early[:, t * TQ : (t + 1) * TQ].indirect(query_list[:]))
 
@@ -61,30 +76,15 @@ def tile_attend_lq_score_kernel(tc, qT, k_words, k_scales, kb, offq, offs, out):
         for r in range(4):
             nc.sync.dma_start(key_scales[:].bitcast(I32)[r:P:32, :], picked_scales[:].bitcast(I32)[32 + 4 * r : 96 : 16, :])
 
-        banks = [ps.tile([P, 4, P], F32, name="spread%d" % g, tag="bank%d" % g) for g in range(RUN // 4)]
-        for j in range(RUN):
-            nc.tensor.transpose(banks[j // 4][:, j % 4, :], bias_runs[:, j : j + 1].to_broadcast([P, P]), ident[:])
-        bias_pool = sb.tile([P, T], F32, name="bias_pool")
-        by_run = bias_pool[:].rearrange("m (p j) -> m p j", j=RUN)
-
-        def lay_out(g):
-            nc.scalar.copy(by_run[:, :, 4 * g : 4 * g + 4], banks[g][:].rearrange("m j p -> m p j"))
-
-        for g in (0, 1):
-            lay_out(g)
         for b in range(B):
             listed = query_list[:, b * NQ // 16 : (b + 1) * NQ // 16]
             nc.vector.tensor_copy(q_picked[:, 2, b * NQ : (b + 1) * NQ], q_late[:, :TQ].indirect(listed))
             nc.scalar.activation(q_picked[:, 3, b * NQ : (b + 1) * NQ], q_late[:, TQ:].indirect(listed), COPY)
         for g in (2, 3):
-            lay_out(g)
-        bias = sb.tile([P, B, N], F32, name="bias")
-        for g in range(2 * B):
-            nc.scalar.activation(
-                bias[:, g // 2, g % 2 * N // 2 : (g % 2 + 1) * N // 2],
-                bias_pool[:].indirect(key_list[:, g * N // 32 : (g + 1) * N // 32]),
-                COPY,
-            )
+            nc.scalar.copy(bias_pool[:, g * N : (g + 1) * N], banks[g][:].rearrange("p j n -> p (j n)"))
+        bias = sb.tile([P, B, N], F32, name="bias", tag="queries_then_bias", align_bytes=ALIGN)
+        for b in range(B):
+            nc.scalar.activation(bias[:, b, :], bias_pool[:].indirect(key_list[:, b * N // 16 : (b + 1) * N // 16]), COPY)
 
         q_grouped = [
             sb.tile([P, NQ, PACK], BF16, name="q_grouped0", tag="grouped_then_words", align_bytes=64),
@@ -124,11 +124,11 @@ def tile_attend_lq_score_kernel(tc, qT, k_words, k_scales, kb, offq, offs, out):
                     stop=True,
                 )
                 scores.append(acc)
-        results = [sb.tile([P, H], F32, name="result%d" % g, align_bytes=ALIGN) for g in range(2 * B)]
-        for i, acc in enumerate(scores):
-            g, lo = divmod(i * WIDTH, H)
-            b, col = divmod(i * WIDTH, N)
-            nc.vector.tensor_tensor(results[g][:, lo : lo + WIDTH], acc[:], bias[:, b, col : col + WIDTH], ADD)
-            if lo + WIDTH == H:
-                queue = nc.sync if g % 2 == 0 else nc.scalar
-                queue.dma_start(out[b, :, col + WIDTH - H : col + WIDTH], results[g][:])
+        store_cuts = [0, WIDTH, H, N, N + H, B * N]
+        for g, (lo, hi) in enumerate(zip(store_cuts, store_cuts[1:])):
+            result = sb.tile([P, hi - lo], F32, name="result%d" % g, align_bytes=ALIGN)
+            b, first = divmod(lo, N)
+            for c in range(lo, hi, WIDTH):
+                nc.vector.tensor_tensor(result[:, c - lo : c - lo + WIDTH], scores[c // WIDTH][:], bias[:, b, c % N : c % N + WIDTH], ADD)
+            queue = nc.sync if g % 2 == 0 else nc.scalar
+            queue.dma_start(out[b, :, first : first + hi - lo], result[:])

@@ -65,11 +65,17 @@ def tile_attend_lq_score_kernel(tc, qT, k_words, k_scales, kb, offq, offs, out):
         for j, column in enumerate(columns):
             nc.tensor.transpose(banks[j // 4][:, j % 4, :], column.to_broadcast([P, P]), ident[:])
         bias_pool = sb.tile([P, T], F32, name="bias_pool")
-        for g in (0, 1):
+
+        def lay_out(g):
             nc.scalar.copy(bias_pool[:, g * N : (g + 1) * N], banks[g][:].rearrange("p j n -> p (j n)"))
+
+        lay_out(0)
+        lay_out(1)
         q_picked = sb.tile([P, PACK, B * NQ], F32, name="q_picked", tag="columns_then_queries")
-        for t in (0, 1):
-            nc.vector.tensor_copy(q_picked[:, t, :], q_early[:, t * TQ : (t + 1) * TQ].indirect(query_list[:]))
+        nc.scalar.activation(q_picked[:, 0, :], q_early[:, :TQ].indirect(query_list[:]), COPY)
+        nc.vector.tensor_copy(q_picked[:, 1, :], q_early[:, TQ:].indirect(query_list[:]))
+
+        lay_out(2)
 
         picked_scales = sb.tile([P, B * N], U8, name="picked_scales", align_bytes=ALIGN)
         nc.vector.tensor_copy(picked_scales[:], scale_pool[:].bitcast(U8).indirect(key_list[:]))
@@ -80,8 +86,7 @@ def tile_attend_lq_score_kernel(tc, qT, k_words, k_scales, kb, offq, offs, out):
             listed = query_list[:, b * NQ // 16 : (b + 1) * NQ // 16]
             nc.vector.tensor_copy(q_picked[:, 2, b * NQ : (b + 1) * NQ], q_late[:, :TQ].indirect(listed))
             nc.scalar.activation(q_picked[:, 3, b * NQ : (b + 1) * NQ], q_late[:, TQ:].indirect(listed), COPY)
-        for g in (2, 3):
-            nc.scalar.copy(bias_pool[:, g * N : (g + 1) * N], banks[g][:].rearrange("p j n -> p (j n)"))
+        lay_out(3)
         bias = sb.tile([P, B, N], F32, name="bias", tag="queries_then_bias", align_bytes=ALIGN)
         for b in range(B):
             nc.scalar.activation(bias[:, b, :], bias_pool[:].indirect(key_list[:, b * N // 16 : (b + 1) * N // 16]), COPY)

@@ -56,10 +56,10 @@ def tile_attend_lq_score_kernel(tc, qT, k_words, k_scales, kb, offq, offs, out):
 
         turned = ps.tile([P, P], F32, name="turned", tag="bank7")
         nc.tensor.transpose(turned[:], bias_rows[:], ident[:])
-        first_cols = sb.tile([P, 12], F32, name="first_cols", tag="columns_then_queries")
-        other_cols = sb.tile([P, 4], F32, name="other_cols")
-        nc.scalar.copy(first_cols[:], turned[:, 48:60])
-        nc.scalar.copy(other_cols[:], turned[:, 60:64])
+        first_cols = sb.tile([P, 8], F32, name="first_cols", tag="columns_then_queries")
+        other_cols = sb.tile([P, 8], F32, name="other_cols")
+        nc.scalar.copy(first_cols[:], turned[:, 48:56])
+        nc.scalar.copy(other_cols[:], turned[:, 56:64])
         columns = [cols[:, j : j + 1] for cols in (first_cols, other_cols) for j in range(cols.shape[1])]
         banks = [ps.tile([P, 4, P], F32, name="spread%d" % g, tag="bank%d" % g) for g in range(RUNS // 4)]
         for j, column in enumerate(columns):
@@ -70,12 +70,11 @@ def tile_attend_lq_score_kernel(tc, qT, k_words, k_scales, kb, offq, offs, out):
             nc.scalar.copy(bias_pool[:, g * N : (g + 1) * N], banks[g][:].rearrange("p j n -> p (j n)"))
 
         lay_out(0)
-        lay_out(1)
         q_picked = sb.tile([P, PACK, B * NQ], F32, name="q_picked", tag="columns_then_queries")
         nc.scalar.activation(q_picked[:, 0, :], q_early[:, :TQ].indirect(query_list[:]), COPY)
         nc.vector.tensor_copy(q_picked[:, 1, :], q_early[:, TQ:].indirect(query_list[:]))
 
-        lay_out(2)
+        lay_out(1)
 
         picked_scales = sb.tile([P, B * N], U8, name="picked_scales", align_bytes=ALIGN)
         nc.vector.tensor_copy(picked_scales[:], scale_pool[:].bitcast(U8).indirect(key_list[:]))
@@ -86,6 +85,7 @@ def tile_attend_lq_score_kernel(tc, qT, k_words, k_scales, kb, offq, offs, out):
             listed = query_list[:, b * NQ // 16 : (b + 1) * NQ // 16]
             nc.vector.tensor_copy(q_picked[:, 2, b * NQ : (b + 1) * NQ], q_late[:, :TQ].indirect(listed))
             nc.scalar.activation(q_picked[:, 3, b * NQ : (b + 1) * NQ], q_late[:, TQ:].indirect(listed), COPY)
+        lay_out(2)
         lay_out(3)
         bias = sb.tile([P, B, N], F32, name="bias", tag="queries_then_bias", align_bytes=ALIGN)
         for b in range(B):

@@ -19,12 +19,14 @@ FP8X4 = mybir.dt.float8_e4m3fn_x4
 ADD = mybir.AluOpType.add
 COPY = mybir.ActivationFunctionType.Copy
 ALIGN = 256
+PICKED_BYTES = 4 * PACK * B * NQ
 
 
 def tile_attend_lq_score_kernel(tc, qT, k_words, k_scales, kb, offq, offs, out):
     nc = tc.nc
     with ExitStack() as ctx:
         sb = ctx.enter_context(tc.tile_pool(name="sb", bufs=1))
+        shared = ctx.enter_context(tc.tile_pool(name="shared", bufs=1))
         ps = ctx.enter_context(tc.psum_pool(name="ps", bufs=1))
 
         key_list = sb.tile([P, B * N // 16], U16, name="key_list", align_bytes=ALIGN)
@@ -56,9 +58,9 @@ def tile_attend_lq_score_kernel(tc, qT, k_words, k_scales, kb, offq, offs, out):
 
         turned = ps.tile([P, P], F32, name="turned", tag="bank7")
         nc.tensor.transpose(turned[:], bias_rows[:], ident[:])
-        first_cols = sb.tile([P, 8], F32, name="first_cols", tag="columns_then_queries")
+        first_cols = shared.tile([P, 16], F32, name="first_cols", offset=PICKED_BYTES - 32)[:, 4:12]
         other_cols = sb.tile([P, 8], F32, name="other_cols")
-        nc.scalar.copy(first_cols[:], turned[:, 48:56])
+        nc.scalar.copy(first_cols, turned[:, 48:56])
         nc.scalar.copy(other_cols[:], turned[:, 56:64])
         columns = [cols[:, j : j + 1] for cols in (first_cols, other_cols) for j in range(cols.shape[1])]
         banks = [ps.tile([P, 4, P], F32, name="spread%d" % g, tag="bank%d" % g) for g in range(RUNS // 4)]
@@ -70,16 +72,17 @@ def tile_attend_lq_score_kernel(tc, qT, k_words, k_scales, kb, offq, offs, out):
             nc.scalar.copy(bias_pool[:, g * N : (g + 1) * N], banks[g][:].rearrange("p j n -> p (j n)"))
 
         lay_out(0)
-        q_picked = sb.tile([P, PACK, B * NQ], F32, name="q_picked", tag="columns_then_queries")
+        picked_scales = shared.tile([P, B * N], U8, name="picked_scales", offset=PICKED_BYTES, align_bytes=ALIGN)
+        nc.vector.tensor_copy(picked_scales[:], scale_pool[:].bitcast(U8).indirect(key_list[:]))
+        q_picked = shared.tile([P, PACK, B * NQ], F32, name="q_picked", offset=0)
         nc.scalar.activation(q_picked[:, 0, :], q_early[:, :TQ].indirect(query_list[:]), COPY)
         nc.vector.tensor_copy(q_picked[:, 1, :], q_early[:, TQ:].indirect(query_list[:]))
 
         lay_out(1)
 
-        picked_scales = sb.tile([P, B * N], U8, name="picked_scales", align_bytes=ALIGN)
-        nc.vector.tensor_copy(picked_scales[:], scale_pool[:].bitcast(U8).indirect(key_list[:]))
-        for r in range(4):
-            nc.sync.dma_start(key_scales[:].bitcast(I32)[r:P:32, :], picked_scales[:].bitcast(I32)[32 + 4 * r : 96 : 16, :])
+        for quad in range(4):
+            queue = nc.sync if quad % 2 == 0 else nc.scalar
+            queue.dma_start(key_scales[:].bitcast(I32)[32 * quad : 32 * quad + 4, :], picked_scales[:].bitcast(I32)[32 + 16 * quad : 48 + 16 * quad : 4, :])
 
         for b in range(B):
             listed = query_list[:, b * NQ // 16 : (b + 1) * NQ // 16]

from contextlib import ExitStack

import concourse.mybir as mybir
from concourse.masks import make_identity

B, N, T, D, NQ, TQ = 2, 512, 2048, 512, 128, 1024
P = 128
PACK = 4
FLOPS = 2 * B * NQ * N * D
BYTES = 4 * D * TQ + D * T + 16 * T + 4 * T + 2 * P * (B * NQ + B * N) // 16 + 4 * B * NQ * N

F32 = mybir.dt.float32
BF16 = mybir.dt.bfloat16
I32 = mybir.dt.int32
U32 = mybir.dt.uint32
U16 = mybir.dt.uint16
U8 = mybir.dt.uint8
FP8X4 = mybir.dt.float8_e4m3fn_x4
ADD = mybir.AluOpType.add
COPY = mybir.ActivationFunctionType.Copy
ALIGN = 256
PICKED_BYTES = 4 * PACK * B * NQ


def tile_attend_lq_score_kernel(tc, qT, k_words, k_scales, kb, offq, offs, out):
    nc = tc.nc
    with ExitStack() as ctx:
        sb = ctx.enter_context(tc.tile_pool(name="sb", bufs=1))
        shared = ctx.enter_context(tc.tile_pool(name="shared", bufs=1))
        ps = ctx.enter_context(tc.psum_pool(name="ps", bufs=1))

        key_list = sb.tile([P, B * N // 16], U16, name="key_list", align_bytes=ALIGN)
        query_list = sb.tile([P, B * NQ // 16], U16, name="query_list", align_bytes=ALIGN)
        q_early = sb.tile([P, 2 * TQ], F32, name="q_early", align_bytes=ALIGN)
        q_late = sb.tile([P, 2 * TQ], F32, name="q_late", tag="queries_then_bias", align_bytes=ALIGN)
        word_pool = sb.tile([P, T], I32, name="word_pool", align_bytes=ALIGN)
        scale_pool = sb.tile([P, T // 4], I32, name="scale_pool", align_bytes=ALIGN)
        RUNS = T // P
        bias_rows = sb.tile([P, P], F32, name="bias_rows", align_bytes=ALIGN)
        ident = sb.tile([P, P], F32, name="ident")
        key_scales = sb.tile([P, B * N], U8, name="key_scales", align_bytes=ALIGN)

        nc.vector.memset(ident[:], 0.0)
        nc.vector.memset(bias_rows[0:48, :], 0.0)
        nc.vector.memset(bias_rows[64:P, :], 0.0)
        nc.vector.memset(scale_pool[:], 0)
        nc.vector.memset(key_scales[:].bitcast(I32), 0)
        make_identity(nc, ident[:], nomemset=True)

        q_rows = qT.rearrange("(p t) n -> p (t n)", t=PACK)
        nc.scalar.dma_start(bias_rows[48:64, :], kb[0].rearrange("(j n) -> j n", n=P))
        nc.sync.dma_start(q_early[:], q_rows[:, : 2 * TQ])
        nc.sync.dma_start(key_list[:], offs)
        nc.sync.dma_start(scale_pool[32:96:4, :], k_scales[0].bitcast(I32))
        nc.sync.dma_start(query_list[:], offq)
        nc.sync.dma_start(q_late[:], q_rows[:, 2 * TQ :])
        nc.sync.dma_start(word_pool[:], k_words[0].rearrange("p t r -> p (t r)").bitcast(I32))

        turned = ps.tile([P, P], F32, name="turned", tag="bank7")
        nc.tensor.transpose(turned[:], bias_rows[:], ident[:])
        first_cols = shared.tile([P, 16], F32, name="first_cols", offset=PICKED_BYTES - 32)[:, 4:12]
        other_cols = sb.tile([P, 8], F32, name="other_cols")
        nc.scalar.copy(first_cols, turned[:, 48:56])
        nc.scalar.copy(other_cols[:], turned[:, 56:64])
        columns = [cols[:, j : j + 1] for cols in (first_cols, other_cols) for j in range(cols.shape[1])]
        banks = [ps.tile([P, 4, P], F32, name="spread%d" % g, tag="bank%d" % g) for g in range(RUNS // 4)]
        for j, column in enumerate(columns):
            nc.tensor.transpose(banks[j // 4][:, j % 4, :], column.to_broadcast([P, P]), ident[:])
        bias_pool = sb.tile([P, T], F32, name="bias_pool")

        def lay_out(g):
            nc.scalar.copy(bias_pool[:, g * N : (g + 1) * N], banks[g][:].rearrange("p j n -> p (j n)"))

        lay_out(0)
        picked_scales = shared.tile([P, B * N], U8, name="picked_scales", offset=PICKED_BYTES, align_bytes=ALIGN)
        nc.vector.tensor_copy(picked_scales[:], scale_pool[:].bitcast(U8).indirect(key_list[:]))
        q_picked = shared.tile([P, PACK, B * NQ], F32, name="q_picked", offset=0)
        nc.scalar.activation(q_picked[:, 0, :], q_early[:, :TQ].indirect(query_list[:]), COPY)
        nc.vector.tensor_copy(q_picked[:, 1, :], q_early[:, TQ:].indirect(query_list[:]))

        lay_out(1)

        for quad in range(4):
            queue = nc.sync if quad % 2 == 0 else nc.scalar
            queue.dma_start(key_scales[:].bitcast(I32)[32 * quad : 32 * quad + 4, :], picked_scales[:].bitcast(I32)[32 + 16 * quad : 48 + 16 * quad : 4, :])

        for b in range(B):
            listed = query_list[:, b * NQ // 16 : (b + 1) * NQ // 16]
            nc.vector.tensor_copy(q_picked[:, 2, b * NQ : (b + 1) * NQ], q_late[:, :TQ].indirect(listed))
            nc.scalar.activation(q_picked[:, 3, b * NQ : (b + 1) * NQ], q_late[:, TQ:].indirect(listed), COPY)
        lay_out(2)
        lay_out(3)
        bias = sb.tile([P, B, N], F32, name="bias", tag="queries_then_bias", align_bytes=ALIGN)
        for b in range(B):
            nc.scalar.activation(bias[:, b, :], bias_pool[:].indirect(key_list[:, b * N // 16 : (b + 1) * N // 16]), COPY)

        q_grouped = [
            sb.tile([P, NQ, PACK], BF16, name="q_grouped0", tag="grouped_then_words", align_bytes=64),
            sb.tile([P, NQ, PACK], BF16, name="q_grouped1", align_bytes=64),
        ]
        for b in range(B):
            nc.vector.tensor_copy(
                q_grouped[b][:].rearrange("p (c i) t -> p c t i", i=4),
                q_picked[:, :, b * NQ : (b + 1) * NQ].rearrange("p t (c i) -> p c t i", i=4),
            )
        q_codes = sb.tile([P, B * NQ], U32, name="q_codes", align_bytes=64)
        q_scales = sb.tile([P, B * NQ], U8, name="q_scales", align_bytes=64)
        for b in range(B):
            nc.vector.quantize_mx(
                out=q_codes[:, b * NQ : (b + 1) * NQ].bitcast(FP8X4),
                scales=q_scales[:, b * NQ : (b + 1) * NQ],
                in_=q_grouped[b][:].rearrange("p n t -> p (n t)"),
            )

        H = N // 2
        WIDTH = 128
        key_words = sb.tile([P, B * N], U32, name="key_words", tag="grouped_then_words", align_bytes=64)
        cuts = list(range(0, B * N + 1, H))
        scores = []
        for lo, hi in zip(cuts, cuts[1:]):
            nc.vector.tensor_copy(key_words[:, lo:hi], word_pool[:].bitcast(U32).indirect(key_list[:, lo // 16 : hi // 16]))
            for c in range(lo, hi, WIDTH):
                b = c // N
                acc = ps.tile([P, WIDTH], F32, name="scores%d" % len(scores), tag="bank%d" % len(scores))
                nc.tensor.matmul_mx(
                    out=acc[:],
                    lhsT=q_codes[:, b * NQ : (b + 1) * NQ].bitcast(FP8X4),
                    lhsT_scale=q_scales[:, b * NQ : (b + 1) * NQ],
                    rhs=key_words[:, c : c + WIDTH].bitcast(FP8X4),
                    rhs_scale=key_scales[:, c : c + WIDTH],
                    start=True,
                    stop=True,
                )
                scores.append(acc)
        store_cuts = [0, WIDTH, H, N, N + H, B * N]
        for g, (lo, hi) in enumerate(zip(store_cuts, store_cuts[1:])):
            result = sb.tile([P, hi - lo], F32, name="result%d" % g, align_bytes=ALIGN)
            b, first = divmod(lo, N)
            for c in range(lo, hi, WIDTH):
                nc.vector.tensor_tensor(result[:, c - lo : c - lo + WIDTH], scores[c // WIDTH][:], bias[:, b, c % N : c % N + WIDTH], ADD)
            queue = nc.sync if g % 2 == 0 else nc.scalar
            queue.dma_start(out[b, :, first : first + hi - lo], result[:])
